import numpy as np, ml_dtypes
CORES = [9,25,41,57]
N = 4
BF = ml_dtypes.bfloat16
S, NM, L, RO, TAU = 2048, 4096, 256, 4, 5
ST, C0, LN = S // L, 16 - RO, NM.bit_length() - 1
def pack(nm, st, kd, ac, fu):
    return np.where(fu, 1 + 2048 * nm + 32 * st + 16 * kd + ac, 0)
def done(e, x, w, kp):
    return {"ent": np.ascontiguousarray(e.reshape(N, 128, S)).astype(np.int32), "feat": np.ascontiguousarray(x.reshape(N, 128, NM)).astype(np.float32).astype(BF),
            "wt": np.ascontiguousarray(w.reshape(N, 128, 1)).astype(np.int32), "kap": np.ascontiguousarray(kp.reshape(N, 128, 1)).astype(np.int32)}
def pooled(rng, n, other):
    pool = rng.integers(0, NM, (8, 16, n)); pool[..., 0] = rng.choice(np.array([0, NM - 1]), (8, 16))
    j = (n * rng.random((N, 8, 16, S)) ** 2).astype(np.int64)
    v = pool[np.arange(8)[:, None, None], np.arange(16)[None, :, None], j]
    return np.where(rng.random(v.shape) < other, rng.integers(0, NM, v.shape), v)
def parts(rng, n, other):
    sh = (N, 8, 16, S); nm = pooled(rng, n, other)
    st = rng.integers(0, 64, sh); kd = (rng.random(sh) < 0.45).astype(np.int64); ac = rng.integers(0, 16, sh); fu = rng.random(sh) < 0.8
    x = (64 * rng.random((N, 8, 16, NM)) ** 2).astype(np.int64)
    return nm, st, kd, ac, fu, x, rng.integers(0, 256, (N, 8, 16)), rng.integers(0, 256, (N, 8, 16))
def setup_inputs(rng):
    nm, st, kd, ac, fu, x, w, kp = parts(rng, 24, 0.3)
    return done(pack(nm, st, kd, ac, fu), x, w, kp)
def setup_inputs_spread(rng):
    sh = (N, 8, 16, S)
    nm = np.exp2(LN * rng.random(sh)).astype(np.int64) - 1; nm = np.where(rng.random((1, 8, 16, 1)) < 0.5, NM - 1 - nm, nm)
    st = np.exp2(6 * rng.random(sh)).astype(np.int64) - 1; st = np.where(rng.random(sh) < 0.5, 63 - st, st)
    kd = (rng.random(sh) < rng.choice(np.array([0.1, 0.4, 0.8]), (N, 8, 1, 1))).astype(np.int64)
    fu = rng.random(sh) < rng.random((N, 8, 1, S))
    x = (np.exp2(6 * rng.random((N, 8, 1, NM))) * rng.random((N, 8, 16, NM))).astype(np.int64)
    w = np.exp2(8 * rng.random((N, 8, 16))).astype(np.int64) - 1; kp = 256 - np.exp2(8 * rng.random((N, 8, 16))).astype(np.int64)
    return done(pack(nm, st, kd, rng.integers(0, 16, sh), fu), x, w, kp)
def at_ends(rng, hi):
    o = np.argsort(rng.random((N, 8, 16)), axis=-1)
    return np.where(o < 11, hi * rng.integers(0, 2, o.shape), rng.integers(0, hi + 1, o.shape))
def setup_inputs_ends(rng):
    sh = (N, 8, 16, S); top = 2048 * NM
    z = 32 * 63 * rng.integers(0, 2, sh) + 15 * rng.integers(0, 2, sh) + 1
    e = np.where(rng.random(sh) < 0.28, 2048 * rng.integers(0, NM, sh) + z, top * rng.integers(0, 2, sh))
    k = rng.random((N, 8, 1, S)); last = 2048 * (NM - 1) + z
    e = np.where(k < 0.41, 16 + z, e); e = np.where(k < 0.37, z, e); e = np.where(k < 0.33, last, e)
    e = np.where(k < 0.26, 0, e); e = np.where(k < 0.16, top, e)
    x = 63 * (rng.random((N, 8, 16, NM)) < 0.2).astype(np.int64); x[..., NM - 1] = 63; x[..., 0] = 0
    w = at_ends(rng, 255); kp = at_ends(rng, 255); w[0, 7] = 255; w[N - 1, 7] = 255
    for c in [0, ST] + list(range(S - ST, S)): e[:, 7, :, c] = last[:, 7, :, c]
    u = 16 * 63 * 255 & 4095
    for m in (8, 15): e[0, 7, :, ((u * u >> 5) + int(kp[N - 1, 7, m]) * u) & (S - 1)] = top
    return done(e, x, w, kp)
def setup_inputs_corners(rng):
    nm, st, kd, ac, fu, x, w, kp = parts(rng, 6, 0.1); sh = kd.shape
    o = rng.permutation(8); md = o[(np.arange(8)[None, :] + (np.arange(N)[:, None] & 1)) & 7]; m4 = md[:, :, None, None]
    kd = np.where(m4 == 0, 1, np.where(m4 == 1, 0, kd)); fu = fu | (m4 == 1)
    fu = np.where(m4 == 2, rng.random((N, 8, 1, S)) < 0.5, fu)
    ac = np.where(m4 == 3, C0 - TAU - 1 + rng.integers(0, RO + 1, sh), ac); kd = np.where(m4 == 3, (rng.random(sh) < 0.7).astype(np.int64), kd)
    st = np.where(m4 == 4, 63 * rng.integers(0, 2, sh), st); st = np.where(m4 == 7, 31, st)
    kd = np.where(m4 == 6, ((np.arange(S)[None, :] & 15) != np.arange(16)[:, None]).astype(np.int64), kd); fu = fu | (m4 == 6)
    x = np.where(m4 == 5, 63, x); m3 = md[:, :, None]
    w = np.where(m3 == 4, 0, np.where(m3 == 7, 255, w)); kp = np.where(m3 == 6, 0, np.where(m3 == 7, 255, kp))
    return done(pack(nm, st, kd, ac, fu), x, w, kp)
def setup_inputs_ties(rng):
    nm, st, kd, ac, fu, x, w, kp = parts(rng, 3, 0.02); sh = st.shape
    st = rng.integers(0, 63, (1, 8, 16, 1)) + rng.integers(0, 2, sh)
    ac = rng.choice(np.array([0, C0 - TAU - 1, C0 - TAU, C0 - TAU + 1, C0, 15]), sh); fu = rng.random(sh) < 0.9
    e = pack(nm, st, kd, ac, fu)
    w[..., 0] |= 1; kp = np.argsort(rng.random((N, 8, 256)), axis=-1)[..., :16]
    nn = rng.integers(0, NM, (N, 8, 16)); c = np.zeros((N, 8, 16), np.int64)
    for r in range(N):
        for g in range(8):
            n = int(nn[r, g, 0])
            if int(np.add.reduce(w[r, g] * x[r, g, :, n])) & 1 == 0: x[r, g, 0, n] ^= 1
            u = int(np.add.reduce(w[r, g] * x[r, g, :, n])) & 4095
            c[r, g] = ((u * u >> 5) + kp[r, g] * u) & (S - 1)
    for r in range(N):
        for g in range(8):
            q = (r + 1) % N; l = min(i for i in range(17) if not np.any(c[r - 1, g] == ST * i))
            s = rng.integers(0, 64, 16); own = pack(nn[r, g], s, (np.arange(16) > 0).astype(np.int64), rng.integers(0, 16, 16), True)
            e[r, g, :, ST * l] = own
            d = rng.integers(1, 4, 16); m = np.sort(rng.permutation(16)[:2]); d[m] = np.array([1, 0]) if (r + g) & 1 else np.array([0, 1])
            miss = np.argsort(rng.random((16, 16)), axis=0) < d[None, :]
            hit = pack(nn[r, g][:, None], s[:, None] ^ rng.integers(1, 64, (16, 16)), rng.integers(0, 2, (16, 16)), rng.integers(0, 16, (16, 16)), True)
            no = np.where(rng.random((16, 16)) < 0.5, 0, (((own - 1) >> 4) << 4)[:, None] + 1 + rng.integers(0, 16, (16, 16)))
            e[q, g][:, c[r, g]] = np.where(miss, no, hit)
    return done(e, x, w, kp)
def gone(v, c):
    return np.where((((37 * c + v) >> 3) & 7) == 0, v ^ 8, v)
def setup_inputs_crowd(rng):
    nm, st, kd, ac, fu, x, w, kp = parts(rng, 8, 0.2)
    e = np.take_along_axis(pack(nm, st, kd, ac, fu), rng.integers(0, 24, (N, 8, 1, S)), 3)
    kp[:, ::2] = kp[:, ::2, :1]
    h = int(rng.integers(0, 8)); kp[:, h] = 0; w[:, h] = 0; w[:, h, 0] = 1; w[:, h, 15] = 64
    cols = ST * np.arange(1, L); sh = (16, L - 1)
    for r in range(N):
        q = (r + 1) % N; o = rng.permutation(4096); c = (o * o >> 5) & (S - 1)
        first = np.unique(c, return_index=True)[1]; first = first[c[first] % ST != 0]
        u = o[rng.permutation(first)[:L - 1]]; p = (u * u >> 5) & (S - 1)
        names = rng.permutation(NM)[:L - 1]; x[r, h, 0, names] = u & 63; x[r, h, 15, names] = u >> 6
        it = rng.random(sh) < 0.4; it[0] = True; it[15] = True
        a = pack(np.where(it, names[None, :], rng.integers(0, NM, sh)), rng.integers(0, 64, sh), 1 - it.astype(np.int64), rng.integers(0, C0 - TAU, sh), True)
        b = pack(gone(rng.integers(0, NM, sh), p[None, :]), rng.integers(0, 64, sh), 1, rng.integers(0, C0 - TAU, sh), True)
        full = rng.random(L - 1) < 0.5; full[-1] = True
        e[r, h][:, cols] = a
        e[q, h][:, p] = np.where(full[None, :], b, a)
    e[:, h, :, 0] = pack(gone(rng.integers(0, NM, 16), 0), rng.integers(0, 64, 16), 1, rng.integers(0, C0 - TAU, 16), True)[None, :]
    return done(e, x, w, kp)
def check_inputs(d):
    bad = []
    for k, lo, hi in (("ent", 0, 2048 * NM), ("feat", 0, 63), ("wt", 0, 255), ("kap", 0, 255)):
        v = np.asarray(d[k]).astype(np.float64)
        if not (np.min(v) >= lo and np.max(v) <= hi): bad.append("range of " + k)
        elif np.any(v != np.floor(v)): bad.append("whole numbers in " + k)
    return bad
def item(a):
    return (a > 0) & ((((a - 1) >> 4) & 1) == 0)
def asleep(a, clock):
    return (a > 0) & ((((a - 1) >> 4) & 1) == 1) & (clock - ((a - 1) & 15) > TAU)
def stay(a, site, clock):
    return np.where(asleep(a, clock) & ((((37 * site + ((a - 1) >> 11)) >> 3) & 7) != 0), 0, a)
def meet(a, b, clock):
    same = (a > 0) & (b > 0) & (((a - 1) >> 11) == ((b - 1) >> 11)); big = np.maximum(a, b)
    wake = same & asleep(big, clock) & item(np.minimum(a, b))
    big = np.where(wake, (((big - 1) >> 4) << 4) + clock + 1, big)
    return np.where(same, big, np.where((a == 0) & ~asleep(b, clock), b, a)), np.where(same, big, np.where((b == 0) & ~asleep(a, clock), a, b))
def reference(ent, feat, wt, kap):
    E = ent.astype(np.int64).reshape(N, 8, 16, S); X = feat.astype(np.float32).astype(np.int64).reshape(N, 8, 16, NM)
    w = wt.astype(np.int64).reshape(N, 8, 16, 1); kp = kap.astype(np.int64).reshape(N, 8, 16, 1); A = [0] * N
    for t in range(RO):
        clock = C0 + t; lane = ST * np.arange(L) + t % ST; new = E.copy(); called = []
        for r in range(N):
            q = (r + 1 + t % (N - 1)) % N
            a = E[r][:, :, lane]
            x = np.take_along_axis(X[r], np.maximum((a - 1) >> 11, 0).reshape(8, 1, 16 * L), 2).reshape(8, 16, 16, L)
            y = np.max(np.where(item(a)[:, None], x, 0), axis=2)
            u = np.add.reduce(w[r] * y, axis=1)[:, None, :] & 4095
            e = ((u * u >> 5) + kp[r] * u + A[r]) & (S - 1)
            cand = np.take_along_axis(E[q], e.reshape(8, 1, 16 * L), 2).reshape(8, 16, 16, L) - 1
            own = a[:, :, None, :] - 1
            score = np.add.reduce((((cand >> 11) == (own >> 11)) & ((cand >> 4) != (own >> 4))).astype(np.int64), axis=1)
            p = np.take_along_axis(e, np.argmax(score, axis=1)[:, None, :], 1)
            win = np.zeros((8, L), bool)
            for g in range(8): win[g, np.unique(p[g, 0], return_index=True)[1]] = True
            b = np.take_along_axis(E[q], p, 2)
            na, nb = meet(stay(a, lane[None, None, :], clock), stay(b, p, clock), clock)
            new[r][:, :, lane] = np.where(win[:, None, :], na, a)
            called.append((q, p[:, 0], win, nb)); A[r] = int(np.count_nonzero(win)) & 31
        for q, p, win, nb in called:
            for g in range(8): new[q, g][:, p[g, win[g]]] = nb[g][:, win[g]]
        E = new
    return {"yent": E.reshape(N, 128, S).astype(np.float32)}

@@ -1,0 +1,556 @@
+from concourse.mybir import AluOpType as OP, ActivationFunctionType as AF
+
+L, S, NM, RO, C0 = 256, 2048, 4096, 4, 12
+SW_ = S + L
+NCH = 8
+CW = 4096 // NCH
+EQV = 9
+CY, WAKE, HOP = 0.00083, 0.1, 3.0
+
+F32, BF, I32, U16, F16 = "float32", "bfloat16", "int32", "uint16", "float16"
+SCRATCH = {}
+PART = {}
+for _buf, _d, _parts in (
+        ("KI", I32, (("pidx pm ai aj", 1), ("c64 c64b", 64), ("k4 k5", 16))),
+        ("KF", F32, (("wtF kapF pmF p0 kcol lc", 1), ("wcol", 2), ("io16 LL P1 P1n t16 u16", 16), ("k1", 128), ("k2", 64), ("k3", 32))),
+        ("TI", I32, (("s1 nm lo1 dm idx TT ui um sq sq5 es e2 wa1 wa2 wn1 wb1 wnb o1 o2", L),)),
+        ("TF", F32, (("wf kc key TK PBf CP bx XH dd dq d2 sm na nb nbc", L),)),
+        ("TB", BF, (("Y lose junk", L),)), ("TU", U16, (("LS", L), ("pl PL", 16)))):
+    _o = 0
+    for _names, _w in _parts:
+        for _n in _names.split():
+            PART[_n] = (_buf, _o, _w)
+            _o += _w
+    SCRATCH[_buf] = ("sbuf", [128, _o], _d)
+for _names, _w, _d in (
+        ("ENT ENT2", S, I32), ("Np OUT", SW_, F32), ("Wp", SW_, I32), ("FA FB", NM + 16, BF), ("PI CC", S, F32),
+        ("wtS kapS", 1, I32), ("CT", 17 * 128, F32), ("ones SEL0", 128, F32), ("WL AC", 512, BF), ("BD", 128, BF), ("SC IX", 2048, BF),
+        ("SWP", 512, F16), ("PB", L, F16), ("pf", 16, F16), ("OR", 4096, F32), ("D A1 B1 IN", 4096, BF)):
+    for _n in _names.split():
+        SCRATCH[_n] = ("sbuf", [128, _w], _d)
+for _n, _m, _w, _d in (("TRI", 16, 16, BF), ("io3", 16, 16, F32), ("EQ", 16, 256, BF), ("EA", 16, 256, BF), ("si", 2, L, I32), ("lo", 2, L, I32),
+                       ("z", 2, L, I32), ("c", 2, L, F32), ("X1", 2, L, F32), ("e0", 2, L, F32), ("M", 2, L, F32)):
+    SCRATCH[_n] = ("sbuf", [128, _m, _w], _d)
+for _n in "ps_u ps_s0 ps_s1 ps_p ps_d".split():
+    SCRATCH[_n] = ("psum", [128, 512], F32)
+for _n in "pA pB pC".split():
+    SCRATCH[_n] = ("psum", [128, 2, L], F32)
+for _t in range(RO):
+    SCRATCH["ab%d" % _t] = ("sbuf", [128, L], F32)
+    SCRATCH["aL%d" % _t] = ("sbuf", [128, L], F32)
+    for _h in range(2):
+        SCRATCH["eb%d%d" % (_t, _h)] = ("sbuf", [128, 4, 32], U16)
+        SCRATCH["eL%d%d" % (_t, _h)] = ("sbuf", [128, L // 2], U16)
+    SCRATCH["nab%d" % _t] = ("sbuf", [128, L + 8], F32)
+    SCRATCH["naL%d" % _t] = ("sbuf", [128, L + 8], F32)
+SEMAPHORES = ["sV", "sS", "sT", "sG", "dEnt", "dFA", "dFB", "dW", "dK", "dY"]
+for _k in ("a%d", "e%d0", "e%d1", "n%d"):
+    for _t in range(RO):
+        SEMAPHORES += ["r" + _k % _t, "l" + _k % _t]
+
+
+def is_psum(b):
+    return b in SCRATCH and SCRATCH[b][0] == "psum"
+
+
+def make_tools(g, T):
+    queue = {"V": g.vector, "S": g.scalar, "T": g.tensor, "G": g, "Y": g.sync}
+    qsem = {"V": "sV", "S": "sS", "T": "sT", "G": "sG"}
+    nodes = []
+    log = {}
+
+    def touch(i, rg, wr):
+        q, comp, deps = nodes[i][0], nodes[i][7], nodes[i][6]
+        for (b, lo, hi) in rg:
+            for (l0, h0, w0, j) in log.get(b, []):
+                if j == i:
+                    continue
+                same = nodes[j][0] == q and comp and nodes[j][7]
+                if is_psum(b) and not same:
+                    deps[j] = True
+                elif is_psum(b) and q == "T":
+                    deps[j] = deps.get(j, False)
+                elif l0 < hi and lo < h0 and (w0 or wr):
+                    deps[j] = True
+
+    def note(i, rg, wr):
+        for (b, lo, hi) in rg:
+            ent = log.setdefault(b, [])
+            if wr and not is_psum(b):
+                ent[:] = [e for e in ent if not (lo <= e[0] and e[1] <= hi)]
+            ent.append((lo, hi, wr, i))
+
+    def run(q, fn, reads, writes, cost, sem=None, inc=1, lat=0.0):
+        nodes.append([q, fn, sem if sem else qsem[q], inc, cost, lat, {}, sem is None])
+        i = len(nodes) - 1
+        touch(i, reads, False)
+        touch(i, writes, True)
+        note(i, reads, False)
+        note(i, writes, True)
+        return i
+
+    def landed(b, s, val, after, lat):
+        nodes.append([None, None, s, val, 0.0, lat, {after: True}, False])
+        note(len(nodes) - 1, [(b, 0, 1 << 20)], True)
+
+    def plan():
+        n = len(nodes)
+        succ = [[] for _ in range(n)]
+        left = [len(nd[6]) for nd in nodes]
+        for i, nd in enumerate(nodes):
+            for j, w in nd[6].items():
+                succ[j].append((i, w))
+        way = [0.0] * n
+        for i in range(n - 1, -1, -1):
+            way[i] = nodes[i][4] + nodes[i][5] + max([way[k] + (WAKE if w else 0.0) for k, w in succ[i]] + [0.0])
+        ready = {q: [] for q in queue}
+        free = {q: 0.0 for q in queue}
+        at = [0.0] * n
+        out = []
+
+        def opened(i):
+            if nodes[i][0] is None:
+                done(i, at[i])
+            else:
+                ready[nodes[i][0]].append(i)
+
+        def done(i, start):
+            fin = start + nodes[i][4]
+            for k, w in succ[i]:
+                if w:
+                    at[k] = max(at[k], fin + nodes[i][5] + (WAKE if nodes[k][0] is not None else 0.0))
+                left[k] -= 1
+                if left[k] == 0:
+                    opened(k)
+        for i in range(n):
+            if not nodes[i][6]:
+                opened(i)
+        while True:
+            best = None
+            for q, lst in ready.items():
+                if not lst:
+                    continue
+                first = min(max(at[i], free[q]) for i in lst)
+                i = max([i for i in lst if max(at[i], free[q]) <= first + 0.02], key=lambda i: (way[i], -i))
+                if best is None or first < best[0]:
+                    best = (first, q, i)
+            if best is None:
+                return out
+            q, i = best[1], best[2]
+            start = max(at[i], free[q])
+            free[q] = start + nodes[i][4]
+            ready[q].remove(i)
+            out.append(i)
+            done(i, start)
+
+    def issue():
+        total, val, know, known = {}, {}, {}, {q: {} for q in queue}
+        for i, nd in enumerate(nodes):
+            if nd[0] is None:
+                total[nd[2]] = total.get(nd[2], 0) + nd[3]
+                val[i], know[i] = total[nd[2]], {}
+        for i in plan():
+            q, fn, s, inc = nodes[i][:4]
+            deps = [j for j, w in nodes[i][6].items() if w]
+            best = {}
+            for j in deps:
+                sj = nodes[j][2]
+                if known[q].get(sj, 0) < val[j]:
+                    best[sj] = max(best.get(sj, 0), val[j])
+            for j in deps:
+                for sk, vk in know[j].items():
+                    if best.get(nodes[j][2]) == val[j] and sk in best and sk != nodes[j][2] and best[sk] <= vk:
+                        del best[sk]
+            for sk, vk in best.items():
+                queue[q].wait_ge(T.sem[sk], vk)
+                known[q][sk] = max(known[q].get(sk, 0), vk)
+            for j in deps:
+                for sk, vk in know[j].items():
+                    known[q][sk] = max(known[q].get(sk, 0), vk)
+            total[s] = total.get(s, 0) + inc
+            val[i] = total[s]
+            ins = fn(queue[q])
+            if ins is not None:
+                ins.then_inc(T.sem[s], inc)
+            know[i] = dict(known[q])
+        for s, x in total.items():
+            if known["G"].get(s, 0) < x:
+                g.wait_ge(T.sem[s], x)
+    return run, landed, issue
+
+
+def rank_program(g, core, T, topo):
+    rank = T.rank_of(core)
+    if rank is None:
+        return
+    run, landed, issue = make_tools(g, T)
+    cores = list(T.cores)
+
+    def size(b):
+        n = 1
+        for d in SCRATCH[b][1][1:]:
+            n *= d
+        return n
+
+    def v(b, lo=0, hi=None, st=1):
+        if b in PART:
+            b, o, w = PART[b]
+            lo, hi = o + lo, o + (w if hi is None else hi)
+        elif len(SCRATCH[b][1]) == 3:
+            return (T[b][:], [(b, 0, size(b))], size(b))
+        hi = size(b) if hi is None else hi
+        return (T[b][:, lo:hi] if st == 1 else T[b][:, lo:hi:st], [(b, lo, hi)], len(range(lo, hi, st)))
+
+    def v3(b, i, lo, hi):
+        m, w = SCRATCH[b][1][1:]
+        if i is None:
+            return (T[b][:, 0:m, lo:hi], [(b, k * w + lo, k * w + hi) for k in range(m)], m * (hi - lo))
+        return (T[b][:, i, lo:hi], [(b, i * w + lo, i * w + hi)], hi - lo)
+
+    def at(b, o):
+        return (T[b][:].indirect(o[0]), [(b, 0, size(b))] + o[1], 16 * o[2], True)
+
+    def isv(x):
+        return isinstance(x, tuple)
+
+    def regs(*xs):
+        out = []
+        for x in xs:
+            if isv(x):
+                out += x[1]
+        return out
+
+    def ap(x):
+        return x[0] if isv(x) else x
+
+    def wide(*xs):
+        return any(SCRATCH[x[1][0][0]][2] in (F32, I32) for x in xs)
+
+    def ts(o, a, s1, op0, s2=None, op1=None):
+        if op1 is None:
+            f = lambda e: e.tensor_scalar(out=o[0], in0=a[0], scalar1=ap(s1), scalar2=None, op0=op0)
+        else:
+            f = lambda e: e.tensor_scalar(out=o[0], in0=a[0], scalar1=ap(s1), scalar2=ap(s2), op0=op0, op1=op1)
+        run("V", f, regs(a, s1, s2), regs(o), 0.05 + max(64, o[2] * (1.0 if wide(o, a) else 0.5)) * CY)
+
+    def tt(o, a, b, op):
+        k = 1.5 if len(a) > 3 else 1.0 if any(is_psum(x[1][0][0]) for x in (a, b)) else 2.0
+        run("V", lambda e: e.tensor_tensor(out=o[0], in0=a[0], in1=b[0], op=op), regs(a, b), regs(o), 0.05 + max(64, o[2] * k) * CY)
+
+    def tc(o, a):
+        f = lambda e: e.tensor_copy(out=o[0], in_=a[0])
+        if len(o) > 3:
+            run("V", f, regs(a) + o[1][1:], o[1][:1], 0.05 + 3.8 * o[2] * CY)
+        else:
+            k = 1.5 if len(a) > 3 else 1.0 if wide(o, a) else 0.5
+            run("V", f, regs(a), regs(o), 0.05 + max(64, o[2] * k) * CY)
+
+    def fill(o, c):
+        run("V", lambda e: e.memset(o[0], c), [], regs(o), 0.05 + o[2] * CY * (1.0 if wide(o) else 0.5))
+
+    def vtr(o, a):
+        run("V", lambda e: e.transpose(out=o[0], in_=a[0]), regs(a), regs(o), 0.05 + o[2] * CY)
+
+    def act(o, a, func, scale=1.0, bias=0.0, accum=None):
+        b0 = ap(bias)
+        if accum is None:
+            f = lambda e: e.activation(out=o[0], in_=a[0], func=func, bias=b0, scale=scale)
+        else:
+            f = lambda e: e.activation(out=o[0], in_=a[0], func=func, bias=b0, scale=scale, accum_out=accum[0])
+        run("S", f, regs(a, bias), regs(o, accum), 0.065 + max(64, o[2] * (1.5 if len(a) > 3 else 1.0)) * CY)
+
+    def mm(o, lT, r, start, stop):
+        k = 4.0 if SCRATCH[lT[1][0][0]][2] == F32 else 1.0
+        run("T", lambda e: e.matmul(out=o[0], lhsT=lT[0], rhs=r[0], start=start, stop=stop), regs(lT, r), regs(o), 0.00071 * k * max(64, o[2]))
+
+    def iota(o, pattern, base, cm):
+        if SCRATCH[o[1][0][0]][2] != I32:
+            f = lambda e: e.iota(o[0], pattern, base, cm, allow_small_or_imprecise_dtypes=True)
+        else:
+            f = lambda e: e.iota(o[0], pattern, base, cm)
+        run("G", f, [], regs(o), 0.13 + 2 * o[2] * CY)
+
+    def asel(o, a, pattern, cmp, base, cm):
+        run("G", lambda e: e.affine_select(out=o[0], in_=a[0], pattern=pattern, compare_op=cmp, fill=0.0, base=base, channel_multiplier=cm), regs(a), regs(o), 0.17 + 2 * o[2] * CY)
+
+    def send(src, dst, to, frm, kind):
+        rid, pid = topo.addr(to)[:2]
+        m = topo.mask(core, to)
+        rs, ls = "r" + kind, "l" + kind
+
+        def f(e):
+            e.remote_dma(out_ap=T[dst][:], in_ap=T[src][:], remote_sem=T.sem[rs], local_sem=T.sem[ls], pid=pid, routing_id=rid, dma_engine_mask=m)
+        i = run("G", f, [(src, 0, size(src))], [], 0.1, sem=ls, inc=len(topo.engines(core, to)))
+        landed(dst, rs, len(topo.engines(frm, core)), i, HOP)
+
+    run("Y", lambda e: e.dma_start(T.ENT[:], T.ent[:]), [], regs(v("ENT")), 0.1, "dEnt", 16, 5.0)
+    run("S", lambda e: e.dma_start(T.wtS[:], T.wt[:]), [], regs(v("wtS")), 0.1, "dW", 16, 2.0)
+    run("S", lambda e: e.dma_start(T.kapS[:], T.kap[:]), [], regs(v("kapS")), 0.1, "dK", 16, 2.0)
+
+    def load(q, buf, par, sem):
+        def f(e):
+            for a in range(4):
+                for h in range(2):
+                    e.dma_start(T[buf][32 * a + 16 * h:32 * a + 16 * h + 16, 0:NM], T.feat[32 * a + 16 * par:32 * a + 16 * par + 16, :]).then_inc(T.sem[sem], 16)
+        run(q, f, [], [(buf, 0, NM)], 0.8, sem, 128, 8.0)
+    load("Y", "FA", 0, "dFA")
+    load("S", "FB", 1, "dFB")
+
+    fill(v("ones"), 1.0)
+    fill(v("FA", NM, NM + 16), 0.0)
+    fill(v("FB", NM, NM + 16), 0.0)
+    fill(v("Np", S, SW_), 0.0)
+    fill(v("Wp", S, SW_), 0)
+    fill(v("OUT", S, SW_), 0.0)
+    fill(v("SC"), 0.0)
+    fill(v("IX"), 0.0)
+    for t in range(RO):
+        fill(v("nab%d" % t, L, L + 8), 0.0)
+
+    def slot(k, n=1):
+        return v("CT", 128 * k, 128 * (k + n))
+    iota(v("pidx"), [[0, 1]], 0, 1)
+    iota(v("c64"), [[37, 64]], 0, 0)
+    iota(v("io3"), [[0, 16], [1, 16]], 0, 0)
+    iota(v("io16"), [[16, 16]], S, 0)
+    for p in range(2):
+        asel(slot(p), v("ones"), [[-32, 4], [0, 2], [-1, 16]], OP.is_equal, -16 * p, 1)
+    for p in range(2):
+        for h in range(2):
+            k = 2 + 2 * (2 * p + h)
+            asel(slot(k), v("ones"), [[-32, 4], [-1000 if p == 0 else 1000, 2], [0, 16]], OP.is_ge, -16 * h - (1000 if p else 0), 1)
+            asel(slot(k + 1), slot(k), [[32, 4], [0, 2], [0, 16]], OP.is_ge, 15 + 16 * h, -1)
+    asel(slot(10), v("ones"), [[-16, 8], [0, 16]], OP.is_ge, 0, 1)
+    asel(slot(11), slot(10), [[16, 8], [0, 16]], OP.is_ge, 15, -1)
+    asel(slot(12), v("ones"), [[-1, 128]], OP.is_equal, 0, 1)
+    for h in range(2):
+        for p in range(2):
+            asel(slot(13 + 2 * h + p), v("ones"), [[-32, 4], [984, 2], [-1, 16]], OP.is_equal, 16 * (p - h) - 1000 * p, 1)
+    iota(v("PI"), [[1, S]], 0, 0)
+    tc(v("wtF"), v("wtS"))
+    tc(v("kapF"), v("kapS"))
+    for p in range(2):
+        mm(v("ps_p", p, p + 1), slot(p), v("wtF"), True, True)
+    tc(v("wcol"), v("ps_p", 0, 2))
+    for p in range(2):
+        for h in range(2):
+            k = 2 * p + h
+            ts(v("WL", 128 * k, 128 * k + 128), slot(2 + 2 * k + 1), v("wcol", p, p + 1), OP.mult)
+    ts(v("pm"), v("pidx"), 15, OP.bitwise_and)
+    tc(v("pmF"), v("pm"))
+    ts(v("p0"), v("pmF"), 0.0, OP.is_equal)
+    ts(v("kcol"), v("pmF"), -2048.0, OP.mult, 15.0 * 2048, OP.add)
+    ts(v("LL"), v("io16"), v("pmF"), OP.add)
+    ts(v("TRI"), v("io3"), v("pmF"), OP.is_gt)
+    ts(v("SEL0"), v("ones"), v("p0"), OP.mult)
+    tc(v("BD"), slot(11))
+    for q in range(8):
+        ts(v("SC", 16 * q, 16 * q + 129 * 15 + 1, 129), v("CT", 128 * 11 + 16 * q, 128 * 11 + 16 * q + 16), 32768.0, OP.mult)
+        tc(v("IX", 16 * q, 16 * q + 129 * 15 + 1, 129), v("CT", 128 * 12 + 16 * q, 128 * 12 + 16 * q + 16))
+    tc(v("SWP"), slot(13, 4))
+    ts(v("c64b"), v("c64"), 63, OP.bitwise_and)
+    ts(v("CC", 0, 64), v("c64b"), 4096.0, OP.mult, -262144.0 - 2033.0, OP.add)
+    n = 64
+    while n < S:
+        act(v("CC", n, 2 * n), v("CC", 0, n), AF.Copy)
+        n *= 2
+
+    ts(v("ENT2"), v("ENT"), 2047, OP.add)
+    ts(v("ENT2"), v("ENT2"), -2048, OP.bitwise_and)
+    tt(v("Np", 0, S), v("ENT"), v("ENT2"), OP.add)
+
+    back = None
+    for t in range(RO):
+        clock = C0 + t
+        thr = clock - 5
+        d = 1 + t % 3
+        to, frm = cores[(rank + d) % 4], cores[(rank - d) % 4]
+        ab, aL, eb, eL, nab, naL = ["%s%d" % (x, t) for x in ("ab", "aL", "eb", "eL", "nab", "naL")]
+        prev = "naL%d" % (t - 1)
+
+        lanes = v("Np", t, S, 8)
+        ts(v("s1"), lanes, -2033, OP.add)
+        act(v(ab), lanes, AF.Copy)
+        send(ab, aL, to, frm, "a%d" % t)
+        ts(v("nm"), v("s1"), 12, OP.arith_shift_right)
+        ts(v("lo1"), v("s1"), 31, OP.bitwise_and)
+        ts(v("dm"), v("lo1"), 16, OP.is_lt, 4096, OP.mult)
+        tt(v("idx"), v("nm"), v("dm"), OP.max)
+        vtr(v("TT"), v("idx"))
+        for b in range(8):
+            o = 128 * (b // 4)
+            tc(v("LS", o + b % 4, o + 128, 4), v("TT", 32 * b, 32 * b + 32))
+        if t:
+            back(t - 1)
+        for s in range(2):
+            lo, hi = 128 * s, 128 * s + 128
+            for k in range(8):
+                for p in range(2):
+                    o = 256 * s + 128 * p
+                    acc = v("AC", o, o + 128)
+                    win = at("FB" if p else "FA", v("LS", lo + 64 * p + 8 * k, lo + 64 * p + 8 * k + 8))
+                    if k == 0:
+                        act(acc, win, AF.Copy)
+                    else:
+                        tt(acc, win, acc, OP.max)
+            for p in range(2):
+                o = 256 * s + 128 * p
+                tt(v("Y", lo + 64 * p, lo + 64 * p + 64), v("AC", o, o + 64), v("AC", o + 64, o + 128), OP.max)
+            for h in range(2):
+                for p in range(2):
+                    k = 2 * p + h
+                    mm(v("ps_u", lo + 64 * h, lo + 64 * h + 64), v("WL", 128 * k, 128 * k + 128), v("Y", lo + 64 * p, lo + 64 * p + 64), p == 0, p == 1)
+            tc(v("ui", lo, hi), v("ps_u", lo, hi))
+            ts(v("um", lo, hi), v("ui", lo, hi), 4095, OP.bitwise_and)
+            tt(v("sq", lo, hi), v("um", lo, hi), v("um", lo, hi), OP.mult)
+            ku = v3("pA", 0, lo, hi)
+            if t:
+                ts(ku, v("um", lo, hi), v("kapF", 0, 1), OP.mult, v(prev, L, L + 1), OP.add)
+            else:
+                ts(ku, v("um", lo, hi), v("kapF", 0, 1), OP.mult)
+            ts(v("sq5", lo, hi), v("sq", lo, hi), 5, OP.arith_shift_right)
+            tt(v("es", lo, hi), v("sq5", lo, hi), ku, OP.add)
+            ts(v("e2", lo, hi), v("es", lo, hi), 2047, OP.bitwise_and)
+            for h in range(2):
+                tc(v3("%s%d" % (eb, s), None, 16 * h, 16 * h + 16), v("e2", lo + 64 * h, lo + 64 * h + 64))
+            send("%s%d" % (eb, s), "%s%d" % (eL, s), to, frm, "e%d%d" % (t, s))
+
+        if t == 0:
+            ts(v("ENT"), v("Np", 0, S), -2049, OP.add)
+            ts(v("Wp", 0, S), v("ENT"), 4, OP.arith_shift_right)
+        else:
+            act(v("Np", t - 1, S, 8), v(prev, 0, L), AF.Copy)
+            ts(v("wn1"), v(prev, 0, L), -2049, OP.add)
+            ts(v("Wp", t - 1, S, 8), v("wn1"), 4, OP.arith_shift_right)
+            tc(at("Np", v("PL")), v("nb"))
+            tc(at("Wp", v("PL")), v("wnb"))
+        ts(v("wa1"), v(aL), -2049, OP.add)
+        ts(v("wa2"), v("wa1"), 4, OP.arith_shift_right)
+        tc(v("wf"), v("wa2"))
+        for m in range(16):
+            act(v("OR", m, 4096, 16), v("wf"), AF.Copy)
+
+        def side(x, k, lo, hi):
+            low, far = v3("lo", k, lo, hi), v3("pA", 1 - k, lo, hi)
+            ts(low, v3("si", k, lo, hi), 31, OP.bitwise_and)
+            ts(v3("z", k, lo, hi), v3("si", k, lo, hi), 7 << 15, OP.bitwise_and)
+            ts(far, low, thr, OP.is_ge, 262144.0, OP.mult)
+            ts(v3("pB", 1 - k, lo, hi), low, 16, OP.is_ge, float(thr), OP.mult)
+            ts(v3("c", k, lo, hi), low, -1.0, OP.mult, float(clock), OP.add)
+            tt(v3("pC", k, lo, hi), v3("z", k, lo, hi), far, OP.is_le)
+            tt(v3("X1", k, lo, hi), x, v3("pC", k, lo, hi), OP.mult)
+            tt(far, x, far, OP.mult)
+            act(v3("e0", k, lo, hi), v3("X1", k, lo, hi), AF.Relu, scale=-2.0 ** -18, bias=2.0 ** -18)
+
+        tt(v3("si", 0, 0, L), v(aL), v("CC", t, S, 8), OP.add)
+        side(v(aL), 0, 0, L)
+        for s in range(2):
+            ts(v("kc", 128 * s, 128 * s + 128), v("%s%d" % (eL, s)), v("kcol", 0, 1), OP.add)
+        for k in range(NCH):
+            lo, hi, n = CW * k, CW * k + CW, CW // 16
+            q = k * n
+            tt(v("D", lo, hi), at("Wp", v("%s%d" % (eL, q // 128), q % 128, q % 128 + n)), v("OR", lo, hi), OP.subtract)
+            act(v("A1", lo, hi), v("D", lo, hi), AF.Abs)
+            act(v("B1", lo, hi), v("A1", lo, hi), AF.Abs, bias=-64.0)
+            ts(v("IN", lo, hi), v("B1", lo, hi), 63.5, OP.is_lt)
+            for m in range(16):
+                mm(v("ps_s%d" % (q // 128), q % 128, q % 128 + n), v("SC", 128 * m, 128 * m + 128), v("IN", lo + m, hi, 16), m == 0, m == 15)
+        for s in range(2):
+            lo, hi = 128 * s, 128 * s + 128
+
+            def f(b, n, o=0, st=1):
+                return v(b, n * s + o, n * s + n, st)
+            tt(f("key", 128), v("ps_s%d" % s, 0, 128), f("kc", 128), OP.add)
+            vtr(f("TK", 128), f("key", 128))
+            tt(f("k1", 64), f("TK", 128, 0, 2), f("TK", 128, 1, 2), OP.max)
+            tt(f("k2", 32), f("k1", 64, 0, 2), f("k1", 64, 1, 2), OP.max)
+            tt(f("k3", 16), f("k2", 32, 0, 2), f("k2", 32, 1, 2), OP.max)
+            tt(f("k4", 8), f("k3", 16, 0, 2), f("k3", 16, 1, 2), OP.max)
+            ts(f("k5", 8), f("k4", 8), 2047, OP.bitwise_and)
+            tc(f("pf", 8), f("k5", 8))
+            for h in range(2):
+                for p in range(2):
+                    k = 2 * h + p
+                    mm(f("ps_p", 8, h, 2), v("SWP", 128 * k, 128 * k + 128), f("pf", 8, p, 2), p == 0, p == 1)
+            tc(f("pl", 8), f("ps_p", 8))
+            act(f("P1", 8), f("ps_p", 8), AF.Copy)
+            act(f("P1n", 8), f("P1", 8), AF.Copy, scale=-1.0)
+            act(f("CP", 128), at("CC", f("pl", 8)), AF.Copy)
+            act(f("bx", 128), at("Np", f("pl", 8)), AF.Copy)
+            tc(f("PB", 128), at("PI", f("pl", 8)))
+            tt(v3("si", 1, lo, hi), at("Np", f("pl", 8)), f("CP", 128), OP.add)
+            side(f("bx", 128), 1, lo, hi)
+            both = v3("pC", None, lo, hi)
+            tt(f("dd", 128), v3("X1", 0, lo, hi), v3("X1", 1, lo, hi), OP.subtract)
+            act(f("dq", 128), f("dd", 128), AF.Square, scale=2.0 ** -11)
+            act(f("d2", 128), f("dq", 128), AF.Relu, scale=-1.0, bias=1.0)
+            act(f("sm", 128), f("d2", 128), AF.Sign)
+            tt(both, v3("lo", None, lo, hi), v3("pB", None, lo, hi), OP.is_lt)
+            tt(both, v3("c", None, lo, hi), both, OP.mult)
+            tt(f("XH", 128), v3("X1", 0, lo, hi), v3("pC", 0, lo, hi), OP.add)
+            big = v3("pC", 1, lo, hi)
+            tt(big, v3("X1", 1, lo, hi), big, OP.add)
+            tt(big, f("XH", 128), big, OP.max)
+            tt(big, f("sm", 128), big, OP.mult)
+            fil = v3("pA", None, lo, hi)
+            tt(fil, v3("e0", None, lo, hi), fil, OP.mult)
+            tt(v3("M", None, lo, hi), v3("X1", None, lo, hi), fil, OP.max)
+        act(v("PBf", 128, L), at("PI", v("pl", 8, 16)), AF.Copy)
+        for c in range(16):
+            n = 256 - 16 * c
+            if c < EQV:
+                ts(v3("EQ", c, 0, n), v("PB", 16 * c, 256), v("P1", c, c + 1), OP.is_equal)
+            else:
+                act(v3("EA", c, 0, n), v("PBf", 16 * c, 256), AF.Abs, bias=v("P1n", c, c + 1))
+                act(v3("EQ", c, 0, n), v3("EA", c, 0, n), AF.Relu, scale=-1.0, bias=1.0)
+        dg = v3("EQ", None, 0, 16)
+        tt(dg, dg, v("TRI"), OP.mult)
+        for c in range(16):
+            mm(v("ps_d", 16 * c, 256), v("BD"), v3("EQ", c, 0, 256 - 16 * c), c == 0, c == 15)
+        act(v("lose"), v("ps_d", 0, 256), AF.Sign, accum=v("lc"))
+        for x in range(16):
+            mm(v("ps_d", 256, 272), v("IX", 128 * x, 128 * x + 128), v("lose", x, 256, 16), x == 0, x == 15)
+        tt(v("t16"), v("LL"), v("ps_d", 256, 272), OP.mult)
+        tt(v("u16"), v("t16"), v("P1"), OP.max)
+        tc(v("PL"), v("u16"))
+        if t < RO - 1:
+            mm(v("ps_p", 32, 33), v("SEL0"), v("lc"), True, True)
+        big = v3("pC", 1, 0, L)
+
+        def back(t, aL=aL, nab=nab, to=to, frm=frm, naL=naL, big=big):
+            df = v3("pB", 1, 0, L)
+            tt(v("na"), v3("M", 0, 0, L), big, OP.max)
+            tt(df, v(aL), v("na"), OP.subtract)
+            tt(df, v("lose"), df, OP.mult)
+            tt(v(nab, 0, L), v("na"), df, OP.add)
+            if t < RO - 1:
+                ts(v("ai", 0, 1), v("ps_p", 32, 33), -1.0, OP.mult)
+                ts(v("aj", 0, 1), v("ai", 0, 1), 31, OP.bitwise_and)
+                tc(v(nab, L, L + 1), v("aj", 0, 1))
+            send(nab, naL, frm, to, "n%d" % t)
+            if t < RO - 1:
+                ts(v("wb1"), v("nb"), -2049, OP.add)
+                ts(v("wnb"), v("wb1"), 4, OP.arith_shift_right)
+
+        if t == RO - 1:
+            back(t)
+        tt(v("nb"), v3("M", 1, 0, L), big, OP.max)
+        if t < RO - 1:
+            tc(at("Np", v("PL")), v("nb"))
+
+    big = 12582912.0
+    for k in range(4):
+        lo, hi = 512 * k, 512 * k + 512
+        act(v("OR", lo, hi), v("Np", lo, hi), AF.Identity, scale=2.0 ** -12, bias=big)
+        act(v("OR", S + lo, S + hi), v("OR", lo, hi), AF.Identity, scale=2048.0, bias=-2048.0 * big)
+        tt(v("OUT", lo, hi), v("Np", lo, hi), v("OR", S + lo, S + hi), OP.subtract)
+
+    def number(o, x):
+        ts(v("o1"), x, 2047, OP.add)
+        ts(v("o2"), v("o1"), 1, OP.arith_shift_right, -2048, OP.bitwise_and)
+        tt(o, x, v("o2"), OP.subtract)
+    number(v("nbc"), v("nb"))
+    number(v("OUT", RO - 1, S, 8), v("naL%d" % (RO - 1), 0, L))
+    tc(at("OUT", v("PL")), v("nbc"))
+    run("Y", lambda e: e.dma_start(T.yent[:], T.OUT[:, 0:S]), regs(v("OUT", 0, S)), [("yent", 0, S)], 0.1, "dY", 16, 6.0)
+    issue()

@@ -4,17 +4,19 @@ L, S, NM, RO, C0 = 256, 2048, 4096, 4, 12
 SW_ = S + L
 NCH = 8
 CW = 4096 // NCH
+NV, WV = 3, 1
+AH1, AH2, AH3 = 6.0, 3.0, 3.0
 EQV = 9
-CY, WAKE, HOP = 0.00083, 0.1, 3.0
+CY, WAKE, HOP, FX = 0.00083, 0.15, 3.5, 0.03
 
 F32, BF, I32, U16, F16 = "float32", "bfloat16", "int32", "uint16", "float16"
 SCRATCH = {}
 PART = {}
 for _buf, _d, _parts in (
-        ("KI", I32, (("pidx pm ai aj", 1), ("c64 c64b", 64), ("k4 k5", 16))),
-        ("KF", F32, (("wtF kapF pmF p0 kcol lc", 1), ("wcol", 2), ("io16 LL P1 P1n t16 u16", 16), ("k1", 128), ("k2", 64), ("k3", 32))),
-        ("TI", I32, (("s1 nm lo1 dm idx TT ui um sq sq5 es e2 wa1 wa2 wn1 wb1 wnb o1 o2", L),)),
-        ("TF", F32, (("wf kc key TK PBf CP bx XH dd dq d2 sm na nb nbc", L),)),
+        ("KI", I32, (("pidx pm", 1), ("c64 c64b", 64), ("k4", L), ("k5", 16))),
+        ("KF", F32, (("wtF kapF pmF p0 kcol lc an aq", 1), ("wcol", 2), ("io16 io1 ucol LL P1 P1n t16 u16", 16))),
+        ("TI", I32, (("s1 lo1 lob sb ui um sq sq5 es e2 o1 o2", L),)),
+        ("TF", F32, (("nf fa fw fl sg sh lo wn wnb wf kc key TK PBf CP bx XH dd dq d2 sm na nb nbc", L),)),
         ("TB", BF, (("Y lose junk", L),)), ("TU", U16, (("LS", L), ("pl PL", 16)))):
     _o = 0
     for _names, _w in _parts:
@@ -23,18 +25,19 @@ for _buf, _d, _parts in (
             _o += _w
     SCRATCH[_buf] = ("sbuf", [128, _o], _d)
 for _names, _w, _d in (
-        ("ENT ENT2", S, I32), ("Np OUT", SW_, F32), ("Wp", SW_, I32), ("FA FB", NM + 16, BF), ("PI CC", S, F32),
-        ("wtS kapS", 1, I32), ("CT", 17 * 128, F32), ("ones SEL0", 128, F32), ("WL AC", 512, BF), ("BD", 128, BF), ("SC IX", 2048, BF),
-        ("SWP", 512, F16), ("PB", L, F16), ("pf", 16, F16), ("OR", 4096, F32), ("D A1 B1 IN", 4096, BF)):
+        ("ENT ENT2", S, I32), ("Np Ip Wp", SW_, F32), ("FA FB", NM + 16, BF), ("PI CC", S, F32),
+        ("wtS kapS", 1, I32), ("CT", 17 * 128, F32), ("ones SEL0", 128, F32), ("WL AC", 512, BF), ("BD", 128, BF), ("SC IX UT", 2048, BF),
+        ("SWP", 512, F16), ("IDH", 128, F16), ("PB idx TT", L, F16), ("ZE", L, BF), ("MK", 128, F32), ("pf", 16, F16), ("OR", 4096, F32), ("D A1 B1 IN", 4096, BF)):
     for _n in _names.split():
         SCRATCH[_n] = ("sbuf", [128, _w], _d)
-for _n, _m, _w, _d in (("TRI", 16, 16, BF), ("io3", 16, 16, F32), ("EQ", 16, 256, BF), ("EA", 16, 256, BF), ("si", 2, L, I32), ("lo", 2, L, I32),
+for _n, _m, _w, _d in (("EQ", 16, 256, BF), ("EA", 16 - EQV, 256 - 16 * EQV, BF), ("si", 2, L, I32),
                        ("z", 2, L, I32), ("c", 2, L, F32), ("X1", 2, L, F32), ("e0", 2, L, F32), ("M", 2, L, F32)):
     SCRATCH[_n] = ("sbuf", [128, _m, _w], _d)
-for _n in "ps_u ps_s0 ps_s1 ps_p ps_d".split():
+for _n in "ps_u ps_s0 ps_s1 ps_d".split():
     SCRATCH[_n] = ("psum", [128, 512], F32)
-for _n in "pA pB pC".split():
-    SCRATCH[_n] = ("psum", [128, 2, L], F32)
+SCRATCH["ps_p"] = ("psum", [128, 32, 16], F32)
+SCRATCH["pA"] = SCRATCH["pB"] = ("psum", [128, 4, L // 2], F32)
+SCRATCH["pC"] = ("psum", [128, 2, L], F32)
 for _t in range(RO):
     SCRATCH["ab%d" % _t] = ("sbuf", [128, L], F32)
     SCRATCH["aL%d" % _t] = ("sbuf", [128, L], F32)
@@ -58,6 +61,7 @@ def make_tools(g, T):
     qsem = {"V": "sV", "S": "sS", "T": "sT", "G": "sG"}
     nodes = []
     log = {}
+    ahead = [0.0]
 
     def touch(i, rg, wr):
         q, comp, deps = nodes[i][0], nodes[i][7], nodes[i][6]
@@ -81,7 +85,7 @@ def make_tools(g, T):
             ent.append((lo, hi, wr, i))
 
     def run(q, fn, reads, writes, cost, sem=None, inc=1, lat=0.0):
-        nodes.append([q, fn, sem if sem else qsem[q], inc, cost, lat, {}, sem is None])
+        nodes.append([q, fn, sem if sem else qsem[q], inc, cost, lat, {}, sem is None, ahead[0]])
         i = len(nodes) - 1
         touch(i, reads, False)
         touch(i, writes, True)
@@ -90,7 +94,7 @@ def make_tools(g, T):
         return i
 
     def landed(b, s, val, after, lat):
-        nodes.append([None, None, s, val, 0.0, lat, {after: True}, False])
+        nodes.append([None, None, s, val, 0.0, lat, {after: True}, False, 0.0])
         note(len(nodes) - 1, [(b, 0, 1 << 20)], True)
 
     def plan():
@@ -103,6 +107,8 @@ def make_tools(g, T):
         way = [0.0] * n
         for i in range(n - 1, -1, -1):
             way[i] = nodes[i][4] + nodes[i][5] + max([way[k] + (WAKE if w else 0.0) for k, w in succ[i]] + [0.0])
+        for i, nd in enumerate(nodes):
+            way[i] += nd[8]
         ready = {q: [] for q in queue}
         free = {q: 0.0 for q in queue}
         at = [0.0] * n
@@ -176,14 +182,14 @@ def make_tools(g, T):
         for s, x in total.items():
             if known["G"].get(s, 0) < x:
                 g.wait_ge(T.sem[s], x)
-    return run, landed, issue
+    return run, landed, issue, ahead
 
 
 def rank_program(g, core, T, topo):
     rank = T.rank_of(core)
     if rank is None:
         return
-    run, landed, issue = make_tools(g, T)
+    run, landed, issue, ahead = make_tools(g, T)
     cores = list(T.cores)
 
     def size(b):
@@ -203,9 +209,13 @@ def rank_program(g, core, T, topo):
 
     def v3(b, i, lo, hi):
         m, w = SCRATCH[b][1][1:]
-        if i is None:
-            return (T[b][:, 0:m, lo:hi], [(b, k * w + lo, k * w + hi) for k in range(m)], m * (hi - lo))
+        if not isinstance(i, int):
+            i0, i1 = (0, m) if i is None else i
+            return (T[b][:, i0:i1, lo:hi], [(b, k * w + lo, k * w + hi) for k in range(i0, i1)], (i1 - i0) * (hi - lo))
         return (T[b][:, i, lo:hi], [(b, i * w + lo, i * w + hi)], hi - lo)
+
+    def vp(lo, hi, st=1):
+        return (T.ps_p[:, 0, lo:hi] if st == 1 else T.ps_p[:, 0, lo:hi:st], [("ps_p", lo, hi)], len(range(lo, hi, st)))
 
     def at(b, o):
         return (T[b][:].indirect(o[0]), [(b, 0, size(b))] + o[1], 16 * o[2], True)
@@ -251,13 +261,16 @@ def rank_program(g, core, T, topo):
     def vtr(o, a):
         run("V", lambda e: e.transpose(out=o[0], in_=a[0]), regs(a), regs(o), 0.05 + o[2] * CY)
 
+    def scan(o, m, a):
+        run("V", lambda e: e.tensor_tensor_scan(out=o[0], data0=m[0], data1=a[0], initial=0.0, op0=OP.mult, op1=OP.max), regs(m, a), regs(o), FX + o[2] * CY)
+
     def act(o, a, func, scale=1.0, bias=0.0, accum=None):
-        b0 = ap(bias)
+        b0, s0 = ap(bias), ap(scale)
         if accum is None:
-            f = lambda e: e.activation(out=o[0], in_=a[0], func=func, bias=b0, scale=scale)
+            f = lambda e: e.activation(out=o[0], in_=a[0], func=func, bias=b0, scale=s0)
         else:
-            f = lambda e: e.activation(out=o[0], in_=a[0], func=func, bias=b0, scale=scale, accum_out=accum[0])
-        run("S", f, regs(a, bias), regs(o, accum), 0.065 + max(64, o[2] * (1.5 if len(a) > 3 else 1.0)) * CY)
+            f = lambda e: e.activation(out=o[0], in_=a[0], func=func, bias=b0, scale=s0, accum_out=accum[0])
+        run("S", f, regs(a, bias, scale), regs(o, accum), 0.065 + max(64, o[2] * (1.5 if len(a) > 3 else 1.0)) * CY)
 
     def mm(o, lT, r, start, stop):
         k = 4.0 if SCRATCH[lT[1][0][0]][2] == F32 else 1.0
@@ -300,8 +313,11 @@ def rank_program(g, core, T, topo):
     fill(v("FA", NM, NM + 16), 0.0)
     fill(v("FB", NM, NM + 16), 0.0)
     fill(v("Np", S, SW_), 0.0)
-    fill(v("Wp", S, SW_), 0)
-    fill(v("OUT", S, SW_), 0.0)
+    fill(v("Wp", S, SW_), 0.0)
+    fill(v("Ip", S, SW_), 0.0)
+    fill(v("ZE"), 0.0)
+    fill(v("MK"), 1.0)
+    fill(v("MK", 0, 128, 16), 0.0)
     fill(v("SC"), 0.0)
     fill(v("IX"), 0.0)
     for t in range(RO):
@@ -311,8 +327,11 @@ def rank_program(g, core, T, topo):
         return v("CT", 128 * k, 128 * (k + n))
     iota(v("pidx"), [[0, 1]], 0, 1)
     iota(v("c64"), [[37, 64]], 0, 0)
-    iota(v("io3"), [[0, 16], [1, 16]], 0, 0)
+    iota(v("io1"), [[1, 16]], 0, 0)
     iota(v("io16"), [[16, 16]], S, 0)
+    asel(slot(10), v("ones"), [[-16, 8], [0, 16]], OP.is_ge, 0, 1)
+    asel(slot(11), slot(10), [[16, 8], [0, 16]], OP.is_ge, 15, -1)
+    asel(slot(12), v("ones"), [[-1, 128]], OP.is_equal, 0, 1)
     for p in range(2):
         asel(slot(p), v("ones"), [[-32, 4], [0, 2], [-1, 16]], OP.is_equal, -16 * p, 1)
     for p in range(2):
@@ -320,9 +339,6 @@ def rank_program(g, core, T, topo):
             k = 2 + 2 * (2 * p + h)
             asel(slot(k), v("ones"), [[-32, 4], [-1000 if p == 0 else 1000, 2], [0, 16]], OP.is_ge, -16 * h - (1000 if p else 0), 1)
             asel(slot(k + 1), slot(k), [[32, 4], [0, 2], [0, 16]], OP.is_ge, 15 + 16 * h, -1)
-    asel(slot(10), v("ones"), [[-16, 8], [0, 16]], OP.is_ge, 0, 1)
-    asel(slot(11), slot(10), [[16, 8], [0, 16]], OP.is_ge, 15, -1)
-    asel(slot(12), v("ones"), [[-1, 128]], OP.is_equal, 0, 1)
     for h in range(2):
         for p in range(2):
             asel(slot(13 + 2 * h + p), v("ones"), [[-32, 4], [984, 2], [-1, 16]], OP.is_equal, 16 * (p - h) - 1000 * p, 1)
@@ -330,8 +346,8 @@ def rank_program(g, core, T, topo):
     tc(v("wtF"), v("wtS"))
     tc(v("kapF"), v("kapS"))
     for p in range(2):
-        mm(v("ps_p", p, p + 1), slot(p), v("wtF"), True, True)
-    tc(v("wcol"), v("ps_p", 0, 2))
+        mm(vp(p, p + 1), slot(p), v("wtF"), True, True)
+    tc(v("wcol"), vp(0, 2))
     for p in range(2):
         for h in range(2):
             k = 2 * p + h
@@ -341,13 +357,16 @@ def rank_program(g, core, T, topo):
     ts(v("p0"), v("pmF"), 0.0, OP.is_equal)
     ts(v("kcol"), v("pmF"), -2048.0, OP.mult, 15.0 * 2048, OP.add)
     ts(v("LL"), v("io16"), v("pmF"), OP.add)
-    ts(v("TRI"), v("io3"), v("pmF"), OP.is_gt)
+    ts(v("ucol"), v("io1"), v("pmF"), OP.is_gt)
+    for x in range(1, 16):
+        act(v("UT", 128 * x, 128 * x + 128), slot(11), AF.Copy, scale=v("ucol", x, x + 1))
     ts(v("SEL0"), v("ones"), v("p0"), OP.mult)
     tc(v("BD"), slot(11))
     for q in range(8):
-        ts(v("SC", 16 * q, 16 * q + 129 * 15 + 1, 129), v("CT", 128 * 11 + 16 * q, 128 * 11 + 16 * q + 16), 32768.0, OP.mult)
+        act(v("SC", 16 * q, 16 * q + 129 * 15 + 1, 129), v("CT", 128 * 11 + 16 * q, 128 * 11 + 16 * q + 16), AF.Copy, scale=32768.0)
         tc(v("IX", 16 * q, 16 * q + 129 * 15 + 1, 129), v("CT", 128 * 12 + 16 * q, 128 * 12 + 16 * q + 16))
     tc(v("SWP"), slot(13, 4))
+    tc(v("IDH"), slot(12))
     ts(v("c64b"), v("c64"), 63, OP.bitwise_and)
     ts(v("CC", 0, 64), v("c64b"), 4096.0, OP.mult, -262144.0 - 2033.0, OP.add)
     n = 64
@@ -355,9 +374,38 @@ def rank_program(g, core, T, topo):
         act(v("CC", n, 2 * n), v("CC", 0, n), AF.Copy)
         n *= 2
 
-    ts(v("ENT2"), v("ENT"), 2047, OP.add)
-    ts(v("ENT2"), v("ENT2"), -2048, OP.bitwise_and)
-    tt(v("Np", 0, S), v("ENT"), v("ENT2"), OP.add)
+    def entries(o, x, tmp):
+        ts(tmp, x, 2047, OP.add)
+        ts(tmp, tmp, -2048, OP.bitwise_and)
+        tt(o, x, tmp, OP.add)
+    entries(v("ab0"), v("ENT", 0, S, 8), v("o1"))
+    for k in range(NV):
+        entries(v("Np", 512 * k, 512 * k + 512), v("ENT", 512 * k, 512 * k + 512), v("ENT2", 512 * k, 512 * k + 512))
+
+    BIG, MID = 12582912.0, 8387584.0
+
+    for k in range(NV, 4):
+        lo, hi = 512 * k, 512 * k + 512
+        num, quo, bank = v("OR", S + lo, S + hi), v("OR", lo, hi), v("ps_u" if k == 2 else "ps_d")
+        tc(num, v("ENT", lo, hi))
+        act(quo, num, AF.Identity, scale=2.0 ** -11, bias=2047 / 4096)
+        act(quo, quo, AF.Identity, bias=BIG)
+        act(bank, quo, AF.Identity, scale=2048.0, bias=-2048.0 * BIG)
+        tt(v("Np", lo, hi), num, bank, OP.add)
+
+    def mid(o, x):
+        act(o, x, AF.Identity, bias=-MID)
+
+    def w_of(o, x, tmp):
+        act(tmp, x, AF.Identity, scale=1 / 16, bias=-2056.5 / 16)
+        act(tmp, tmp, AF.Identity, bias=BIG)
+        act(o, tmp, AF.Identity, bias=MID / 16 - BIG)
+
+    def n32_of(o, x, tmp):
+        act(tmp, x, AF.Identity, scale=1 / 32, bias=-2048.5 / 32)
+        act(tmp, tmp, AF.Identity, bias=BIG)
+        act(tmp, tmp, AF.Identity, bias=-BIG)
+        act(o, tmp, AF.Identity, scale=32.0, bias=MID + 2033)
 
     back = None
     for t in range(RO):
@@ -368,22 +416,27 @@ def rank_program(g, core, T, topo):
         ab, aL, eb, eL, nab, naL = ["%s%d" % (x, t) for x in ("ab", "aL", "eb", "eL", "nab", "naL")]
         prev = "naL%d" % (t - 1)
 
-        lanes = v("Np", t, S, 8)
+        lanes = v("Np", t, S, 8) if t else v("ab0")
         ts(v("s1"), lanes, -2033, OP.add)
-        act(v(ab), lanes, AF.Copy)
+        act(v("nf"), lanes, AF.Identity, scale=2.0 ** -12, bias=BIG)
+        act(v("nf"), v("nf"), AF.Identity, bias=-BIG - 1 - 2048)
+        if t:
+            act(v(ab), lanes, AF.Copy)
         send(ab, aL, to, frm, "a%d" % t)
-        ts(v("nm"), v("s1"), 12, OP.arith_shift_right)
         ts(v("lo1"), v("s1"), 31, OP.bitwise_and)
-        ts(v("dm"), v("lo1"), 16, OP.is_lt, 4096, OP.mult)
-        tt(v("idx"), v("nm"), v("dm"), OP.max)
+        dm = v3("pC", 0, 0, L)
+        ts(dm, v("lo1"), 16, OP.is_lt, 8192.0, OP.mult)
+        tt(v("idx"), v("nf"), dm, OP.add)
         vtr(v("TT"), v("idx"))
         for b in range(8):
-            o = 128 * (b // 4)
-            tc(v("LS", o + b % 4, o + 128, 4), v("TT", 32 * b, 32 * b + 32))
+            mm(v("ps_s%d" % (b // 4), b % 4, 128, 4), v("IDH"), v("TT", 32 * b, 32 * b + 32), True, True)
+        for s in range(2):
+            ts(v("LS", 128 * s, 128 * s + 128), v("ps_s%d" % s, 0, 128), 2048.0, OP.add, 4096.0, OP.min)
         if t:
             back(t - 1)
         for s in range(2):
             lo, hi = 128 * s, 128 * s + 128
+            ahead[0] = AH1 if s == 0 else 0.0
             for k in range(8):
                 for p in range(2):
                     o = 256 * s + 128 * p
@@ -403,7 +456,7 @@ def rank_program(g, core, T, topo):
             tc(v("ui", lo, hi), v("ps_u", lo, hi))
             ts(v("um", lo, hi), v("ui", lo, hi), 4095, OP.bitwise_and)
             tt(v("sq", lo, hi), v("um", lo, hi), v("um", lo, hi), OP.mult)
-            ku = v3("pA", 0, lo, hi)
+            ku = v3("pC", 0, lo, hi)
             if t:
                 ts(ku, v("um", lo, hi), v("kapF", 0, 1), OP.mult, v(prev, L, L + 1), OP.add)
             else:
@@ -414,41 +467,55 @@ def rank_program(g, core, T, topo):
             for h in range(2):
                 tc(v3("%s%d" % (eb, s), None, 16 * h, 16 * h + 16), v("e2", lo + 64 * h, lo + 64 * h + 64))
             send("%s%d" % (eb, s), "%s%d" % (eL, s), to, frm, "e%d%d" % (t, s))
+            ahead[0] = 0.0
 
         if t == 0:
-            ts(v("ENT"), v("Np", 0, S), -2049, OP.add)
-            ts(v("Wp", 0, S), v("ENT"), 4, OP.arith_shift_right)
+            for k in range(WV):
+                lo, hi = 512 * k, 512 * k + 512
+                ts(v("ENT", lo, hi), v("Np", lo, hi), -2049, OP.add)
+                ts(v("ENT2", lo, hi), v("ENT", lo, hi), 4, OP.arith_shift_right)
+                ts(v("Wp", lo, hi), v("ENT2", lo, hi), -128.0, OP.max)
+            for k in range(WV, 4):
+                lo, hi = 512 * k, 512 * k + 512
+                mid(v("OR", lo, hi), v("Np", lo, hi))
+                w_of(v("Wp", lo, hi), v("OR", lo, hi), v("OR", lo, hi))
         else:
             act(v("Np", t - 1, S, 8), v(prev, 0, L), AF.Copy)
-            ts(v("wn1"), v(prev, 0, L), -2049, OP.add)
-            ts(v("Wp", t - 1, S, 8), v("wn1"), 4, OP.arith_shift_right)
+            mid(v("wn"), v(prev, 0, L))
+            w_of(v("Wp", t - 1, S, 8), v("wn"), v("wn"))
             tc(at("Np", v("PL")), v("nb"))
             tc(at("Wp", v("PL")), v("wnb"))
-        ts(v("wa1"), v(aL), -2049, OP.add)
-        ts(v("wa2"), v("wa1"), 4, OP.arith_shift_right)
-        tc(v("wf"), v("wa2"))
+        mid(v("fa"), v(aL))
+        w_of(v("wf"), v("fa"), v("fw"))
         for m in range(16):
             act(v("OR", m, 4096, 16), v("wf"), AF.Copy)
 
-        def side(x, k, lo, hi):
-            low, far = v3("lo", k, lo, hi), v3("pA", 1 - k, lo, hi)
-            ts(low, v3("si", k, lo, hi), 31, OP.bitwise_and)
-            ts(v3("z", k, lo, hi), v3("si", k, lo, hi), 7 << 15, OP.bitwise_and)
-            ts(far, low, thr, OP.is_ge, 262144.0, OP.mult)
-            ts(v3("pB", 1 - k, lo, hi), low, 16, OP.is_ge, float(thr), OP.mult)
-            ts(v3("c", k, lo, hi), low, -1.0, OP.mult, float(clock), OP.add)
+        def side(x, k, s):
+            lo, hi = 128 * s, 128 * s + 128
+            far = v3("pB" if s else "pA", 1 - k, 0, 128)
             tt(v3("pC", k, lo, hi), v3("z", k, lo, hi), far, OP.is_le)
             tt(v3("X1", k, lo, hi), x, v3("pC", k, lo, hi), OP.mult)
             tt(far, x, far, OP.mult)
             act(v3("e0", k, lo, hi), v3("X1", k, lo, hi), AF.Relu, scale=-2.0 ** -18, bias=2.0 ** -18)
 
-        tt(v3("si", 0, 0, L), v(aL), v("CC", t, S, 8), OP.add)
-        side(v(aL), 0, 0, L)
+        act(v("ps_s0", L, 2 * L), v("CC", t, S, 8), AF.Copy)
+        tt(v3("si", 0, 0, L), v(aL), v("ps_s0", L, 2 * L), OP.add)
+        ts(v3("z", 0, 0, L), v3("si", 0, 0, L), 7 << 15, OP.bitwise_and)
+        n32_of(v("ps_d", L, 2 * L), v("fa"), v("fl"))
+        tt(v("lo"), v(aL), v("ps_d", L, 2 * L), OP.subtract)
+        act(v("sg"), v("lo"), AF.Sign, bias=0.5 - thr)
+        act(v("sh"), v("lo"), AF.Sign, bias=-15.5)
+        act(v3("c", 0, 0, L), v("lo"), AF.Identity, scale=-1.0, bias=float(clock))
+        for s in range(2):
+            act(v3("pB" if s else "pA", 1, 0, 128), v("sg", 128 * s, 128 * s + 128), AF.Relu, scale=262144.0)
+            act(v3("pB" if s else "pA", 3, 0, 128), v("sh", 128 * s, 128 * s + 128), AF.Relu, scale=float(thr))
+            side(v(aL, 128 * s, 128 * s + 128), 0, s)
         for s in range(2):
             ts(v("kc", 128 * s, 128 * s + 128), v("%s%d" % (eL, s)), v("kcol", 0, 1), OP.add)
         for k in range(NCH):
             lo, hi, n = CW * k, CW * k + CW, CW // 16
             q = k * n
+            ahead[0] = AH2 if k < NCH // 2 else 0.0
             tt(v("D", lo, hi), at("Wp", v("%s%d" % (eL, q // 128), q % 128, q % 128 + n)), v("OR", lo, hi), OP.subtract)
             act(v("A1", lo, hi), v("D", lo, hi), AF.Abs)
             act(v("B1", lo, hi), v("A1", lo, hi), AF.Abs, bias=-64.0)
@@ -457,56 +524,65 @@ def rank_program(g, core, T, topo):
                 mm(v("ps_s%d" % (q // 128), q % 128, q % 128 + n), v("SC", 128 * m, 128 * m + 128), v("IN", lo + m, hi, 16), m == 0, m == 15)
         for s in range(2):
             lo, hi = 128 * s, 128 * s + 128
+            ahead[0] = AH3 if s == 0 else 0.0
 
             def f(b, n, o=0, st=1):
                 return v(b, n * s + o, n * s + n, st)
             tt(f("key", 128), v("ps_s%d" % s, 0, 128), f("kc", 128), OP.add)
             vtr(f("TK", 128), f("key", 128))
-            tt(f("k1", 64), f("TK", 128, 0, 2), f("TK", 128, 1, 2), OP.max)
-            tt(f("k2", 32), f("k1", 64, 0, 2), f("k1", 64, 1, 2), OP.max)
-            tt(f("k3", 16), f("k2", 32, 0, 2), f("k2", 32, 1, 2), OP.max)
-            tt(f("k4", 8), f("k3", 16, 0, 2), f("k3", 16, 1, 2), OP.max)
-            ts(f("k5", 8), f("k4", 8), 2047, OP.bitwise_and)
+            scan(f("k4", 128), v("MK"), f("TK", 128))
+            ts(f("k5", 8), f("k4", 128, 15, 16), 2047, OP.bitwise_and)
             tc(f("pf", 8), f("k5", 8))
             for h in range(2):
                 for p in range(2):
                     k = 2 * h + p
-                    mm(f("ps_p", 8, h, 2), v("SWP", 128 * k, 128 * k + 128), f("pf", 8, p, 2), p == 0, p == 1)
-            tc(f("pl", 8), f("ps_p", 8))
-            act(f("P1", 8), f("ps_p", 8), AF.Copy)
+                    mm(vp(8 * s + h, 8 * s + 8, 2), v("SWP", 128 * k, 128 * k + 128), f("pf", 8, p, 2), p == 0, p == 1)
+            tc(f("pl", 8), vp(8 * s, 8 * s + 8))
+            act(f("P1", 8), vp(8 * s, 8 * s + 8), AF.Copy)
             act(f("P1n", 8), f("P1", 8), AF.Copy, scale=-1.0)
             act(f("CP", 128), at("CC", f("pl", 8)), AF.Copy)
             act(f("bx", 128), at("Np", f("pl", 8)), AF.Copy)
             tc(f("PB", 128), at("PI", f("pl", 8)))
+            P, low = "pB" if s else "pA", f("lob", 128)
             tt(v3("si", 1, lo, hi), at("Np", f("pl", 8)), f("CP", 128), OP.add)
-            side(f("bx", 128), 1, lo, hi)
-            both = v3("pC", None, lo, hi)
-            tt(f("dd", 128), v3("X1", 0, lo, hi), v3("X1", 1, lo, hi), OP.subtract)
+            ts(low, v3("si", 1, lo, hi), 31, OP.bitwise_and)
+            ts(v3("z", 1, lo, hi), v3("si", 1, lo, hi), 7 << 15, OP.bitwise_and)
+            ts(v3(P, 0, 0, 128), low, thr, OP.is_ge, 262144.0, OP.mult)
+            ts(v3(P, 2, 0, 128), low, 16, OP.is_ge, float(thr), OP.mult)
+            ts(v3("c", 1, lo, hi), low, -1.0, OP.mult, float(clock), OP.add)
+            side(f("bx", 128), 1, s)
+            a = v3("X1", 0, lo, hi)
+            tt(f("dd", 128), a, f("bx", 128), OP.subtract)
             act(f("dq", 128), f("dd", 128), AF.Square, scale=2.0 ** -11)
-            act(f("d2", 128), f("dq", 128), AF.Relu, scale=-1.0, bias=1.0)
-            act(f("sm", 128), f("d2", 128), AF.Sign)
-            tt(both, v3("lo", None, lo, hi), v3("pB", None, lo, hi), OP.is_lt)
+            ts(f("sm", 128), f("dq", 128), 1.0, OP.is_lt)
+            tt(f("sm", 128), f("sm", 128), v3("pC", 1, lo, hi), OP.mult)
+            both, big = v3(P, (2, 4), 0, 128), v3(P, 3, 0, 128)
+            tt(v3(P, 2, 0, 128), f("lo", 128), v3(P, 2, 0, 128), OP.is_lt)
+            tt(big, low, big, OP.is_lt)
             tt(both, v3("c", None, lo, hi), both, OP.mult)
-            tt(f("XH", 128), v3("X1", 0, lo, hi), v3("pC", 0, lo, hi), OP.add)
-            big = v3("pC", 1, lo, hi)
-            tt(big, v3("X1", 1, lo, hi), big, OP.add)
+            tt(f("XH", 128), a, v3(P, 2, 0, 128), OP.add)
+            tt(big, f("bx", 128), big, OP.add)
             tt(big, f("XH", 128), big, OP.max)
             tt(big, f("sm", 128), big, OP.mult)
-            fil = v3("pA", None, lo, hi)
+            fil = v3(P, (0, 2), 0, 128)
             tt(fil, v3("e0", None, lo, hi), fil, OP.mult)
             tt(v3("M", None, lo, hi), v3("X1", None, lo, hi), fil, OP.max)
+            tt(f("nb", 128), v3("M", 1, lo, hi), big, OP.max)
+        ahead[0] = 0.0
         act(v("PBf", 128, L), at("PI", v("pl", 8, 16)), AF.Copy)
         for c in range(16):
             n = 256 - 16 * c
             if c < EQV:
                 ts(v3("EQ", c, 0, n), v("PB", 16 * c, 256), v("P1", c, c + 1), OP.is_equal)
             else:
-                act(v3("EA", c, 0, n), v("PBf", 16 * c, 256), AF.Abs, bias=v("P1n", c, c + 1))
-                act(v3("EQ", c, 0, n), v3("EA", c, 0, n), AF.Relu, scale=-1.0, bias=1.0)
-        dg = v3("EQ", None, 0, 16)
-        tt(dg, dg, v("TRI"), OP.mult)
-        for c in range(16):
-            mm(v("ps_d", 16 * c, 256), v("BD"), v3("EQ", c, 0, 256 - 16 * c), c == 0, c == 15)
+                act(v3("EA", c - EQV, 0, n), v("PBf", 16 * c, 256), AF.Abs, bias=v("P1n", c, c + 1))
+                act(v3("EQ", c, 0, n), v3("EA", c - EQV, 0, n), AF.Relu, scale=-1.0, bias=1.0)
+        mm(v("ps_d", 0, 256), v("BD"), v("ZE"), True, False)
+        for c in range(15):
+            mm(v("ps_d", 16 * c + 16, 256), v("BD"), v3("EQ", c, 16, 256 - 16 * c), False, False)
+        for x in range(1, 16):
+            col = (T.EQ[:, 0:16, x], [("EQ", 256 * c + x, 256 * c + x + 1) for c in range(16)], 16)
+            mm(v("ps_d", x, 256, 16), v("UT", 128 * x, 128 * x + 128), col, False, x == 15)
         act(v("lose"), v("ps_d", 0, 256), AF.Sign, accum=v("lc"))
         for x in range(16):
             mm(v("ps_d", 256, 272), v("IX", 128 * x, 128 * x + 128), v("lose", x, 256, 16), x == 0, x == 15)
@@ -514,43 +590,44 @@ def rank_program(g, core, T, topo):
         tt(v("u16"), v("t16"), v("P1"), OP.max)
         tc(v("PL"), v("u16"))
         if t < RO - 1:
-            mm(v("ps_p", 32, 33), v("SEL0"), v("lc"), True, True)
-        big = v3("pC", 1, 0, L)
+            mm(v3("ps_p", 2, 0, 1), v("SEL0"), v("lc"), True, True)
 
-        def back(t, aL=aL, nab=nab, to=to, frm=frm, naL=naL, big=big):
-            df = v3("pB", 1, 0, L)
-            tt(v("na"), v3("M", 0, 0, L), big, OP.max)
-            tt(df, v(aL), v("na"), OP.subtract)
-            tt(df, v("lose"), df, OP.mult)
-            tt(v(nab, 0, L), v("na"), df, OP.add)
+        def back(t, aL=aL, nab=nab, to=to, frm=frm, naL=naL):
+            na, df = v3("pC", 0, 0, L), v3("pC", 1, 0, L)
+            for s in range(2):
+                tt(v3("pC", 0, 128 * s, 128 * s + 128), v3("M", 0, 128 * s, 128 * s + 128), v3("pB" if s else "pA", 3, 0, 128), OP.max)
+            tt(df, v(aL), na, OP.subtract)
+            tt(v("na"), v("lose"), df, OP.mult)
+            tt(v(nab, 0, L), v("na"), na, OP.add)
             if t < RO - 1:
-                ts(v("ai", 0, 1), v("ps_p", 32, 33), -1.0, OP.mult)
-                ts(v("aj", 0, 1), v("ai", 0, 1), 31, OP.bitwise_and)
-                tc(v(nab, L, L + 1), v("aj", 0, 1))
+                act(v("an"), v3("ps_p", 2, 0, 1), AF.Copy, scale=-1.0)
+                act(v("aq"), v("an"), AF.Identity, scale=1 / 32, bias=-15.5 / 32)
+                act(v("aq"), v("aq"), AF.Identity, bias=BIG)
+                act(v("aq"), v("aq"), AF.Identity, bias=-BIG)
+                act(v(nab, L, L + 1), v("aq"), AF.Identity, scale=-32.0, bias=v("an"))
             send(nab, naL, frm, to, "n%d" % t)
             if t < RO - 1:
-                ts(v("wb1"), v("nb"), -2049, OP.add)
-                ts(v("wnb"), v("wb1"), 4, OP.arith_shift_right)
+                mid(v("wn"), v("nb"))
+                w_of(v("wnb"), v("wn"), v("wn"))
 
         if t == RO - 1:
             back(t)
-        tt(v("nb"), v3("M", 1, 0, L), big, OP.max)
-        if t < RO - 1:
+        else:
             tc(at("Np", v("PL")), v("nb"))
 
-    big = 12582912.0
     for k in range(4):
         lo, hi = 512 * k, 512 * k + 512
-        act(v("OR", lo, hi), v("Np", lo, hi), AF.Identity, scale=2.0 ** -12, bias=big)
-        act(v("OR", S + lo, S + hi), v("OR", lo, hi), AF.Identity, scale=2048.0, bias=-2048.0 * big)
-        tt(v("OUT", lo, hi), v("Np", lo, hi), v("OR", S + lo, S + hi), OP.subtract)
+        bank = v(("ps_u", "ps_s0", "ps_s1", "ps_u")[k])
+        act(v("OR", lo, hi), v("Np", lo, hi), AF.Identity, scale=2.0 ** -12, bias=BIG)
+        act(bank, v("OR", lo, hi), AF.Identity, scale=2048.0, bias=-2048.0 * BIG)
+        tt(v("Ip", lo, hi), v("Np", lo, hi), bank, OP.subtract)
 
     def number(o, x):
         ts(v("o1"), x, 2047, OP.add)
         ts(v("o2"), v("o1"), 1, OP.arith_shift_right, -2048, OP.bitwise_and)
         tt(o, x, v("o2"), OP.subtract)
     number(v("nbc"), v("nb"))
-    number(v("OUT", RO - 1, S, 8), v("naL%d" % (RO - 1), 0, L))
-    tc(at("OUT", v("PL")), v("nbc"))
-    run("Y", lambda e: e.dma_start(T.yent[:], T.OUT[:, 0:S]), regs(v("OUT", 0, S)), [("yent", 0, S)], 0.1, "dY", 16, 6.0)
+    number(v("Ip", RO - 1, S, 8), v("naL%d" % (RO - 1), 0, L))
+    tc(at("Ip", v("PL")), v("nbc"))
+    run("Y", lambda e: e.dma_start(T.yent[:], T.Ip[:, 0:S]), regs(v("Ip", 0, S)), [("yent", 0, S)], 0.1, "dY", 16, 6.0)
     issue()

from concourse.mybir import AluOpType as OP, ActivationFunctionType as AF

L, S, NM, RO, C0 = 256, 2048, 4096, 4, 12
SW_ = S + L
NCH = 8
CW = 4096 // NCH
NV, WV = 3, 1
AH1, AH2, AH3 = 6.0, 3.0, 3.0
EQV = 9
CY, WAKE, HOP, FX = 0.00083, 0.15, 3.5, 0.03

F32, BF, I32, U16, F16 = "float32", "bfloat16", "int32", "uint16", "float16"
SCRATCH = {}
PART = {}
for _buf, _d, _parts in (
        ("KI", I32, (("pidx pm", 1), ("c64 c64b", 64), ("k4", L), ("k5", 16))),
        ("KF", F32, (("wtF kapF pmF p0 kcol lc an aq", 1), ("wcol", 2), ("io16 io1 ucol LL P1 P1n t16 u16", 16))),
        ("TI", I32, (("s1 lo1 lob sb ui um sq sq5 es e2 o1 o2", L),)),
        ("TF", F32, (("nf fa fw fl sg sh lo wn wnb wf kc key TK PBf CP bx XH dd dq d2 sm na nb nbc", L),)),
        ("TB", BF, (("Y lose junk", L),)), ("TU", U16, (("LS", L), ("pl PL", 16)))):
    _o = 0
    for _names, _w in _parts:
        for _n in _names.split():
            PART[_n] = (_buf, _o, _w)
            _o += _w
    SCRATCH[_buf] = ("sbuf", [128, _o], _d)
for _names, _w, _d in (
        ("ENT ENT2", S, I32), ("Np Ip Wp", SW_, F32), ("FA FB", NM + 16, BF), ("PI CC", S, F32),
        ("wtS kapS", 1, I32), ("CT", 17 * 128, F32), ("ones SEL0", 128, F32), ("WL AC", 512, BF), ("BD", 128, BF), ("SC IX UT", 2048, BF),
        ("SWP", 512, F16), ("IDH", 128, F16), ("PB idx TT", L, F16), ("ZE", L, BF), ("MK", 128, F32), ("pf", 16, F16), ("OR", 4096, F32), ("D A1 B1 IN", 4096, BF)):
    for _n in _names.split():
        SCRATCH[_n] = ("sbuf", [128, _w], _d)
for _n, _m, _w, _d in (("EQ", 16, 256, BF), ("EA", 16 - EQV, 256 - 16 * EQV, BF), ("si", 2, L, I32),
                       ("z", 2, L, I32), ("c", 2, L, F32), ("X1", 2, L, F32), ("e0", 2, L, F32), ("M", 2, L, F32)):
    SCRATCH[_n] = ("sbuf", [128, _m, _w], _d)
for _n in "ps_u ps_s0 ps_s1 ps_d".split():
    SCRATCH[_n] = ("psum", [128, 512], F32)
SCRATCH["ps_p"] = ("psum", [128, 32, 16], F32)
SCRATCH["pA"] = SCRATCH["pB"] = ("psum", [128, 4, L // 2], F32)
SCRATCH["pC"] = ("psum", [128, 2, L], F32)
for _t in range(RO):
    SCRATCH["ab%d" % _t] = ("sbuf", [128, L], F32)
    SCRATCH["aL%d" % _t] = ("sbuf", [128, L], F32)
    for _h in range(2):
        SCRATCH["eb%d%d" % (_t, _h)] = ("sbuf", [128, 4, 32], U16)
        SCRATCH["eL%d%d" % (_t, _h)] = ("sbuf", [128, L // 2], U16)
    SCRATCH["nab%d" % _t] = ("sbuf", [128, L + 8], F32)
    SCRATCH["naL%d" % _t] = ("sbuf", [128, L + 8], F32)
SEMAPHORES = ["sV", "sS", "sT", "sG", "dEnt", "dFA", "dFB", "dW", "dK", "dY"]
for _k in ("a%d", "e%d0", "e%d1", "n%d"):
    for _t in range(RO):
        SEMAPHORES += ["r" + _k % _t, "l" + _k % _t]


def is_psum(b):
    return b in SCRATCH and SCRATCH[b][0] == "psum"


def make_tools(g, T):
    queue = {"V": g.vector, "S": g.scalar, "T": g.tensor, "G": g, "Y": g.sync}
    qsem = {"V": "sV", "S": "sS", "T": "sT", "G": "sG"}
    nodes = []
    log = {}
    ahead = [0.0]

    def touch(i, rg, wr):
        q, comp, deps = nodes[i][0], nodes[i][7], nodes[i][6]
        for (b, lo, hi) in rg:
            for (l0, h0, w0, j) in log.get(b, []):
                if j == i:
                    continue
                same = nodes[j][0] == q and comp and nodes[j][7]
                if is_psum(b) and not same:
                    deps[j] = True
                elif is_psum(b) and q == "T":
                    deps[j] = deps.get(j, False)
                elif l0 < hi and lo < h0 and (w0 or wr):
                    deps[j] = True

    def note(i, rg, wr):
        for (b, lo, hi) in rg:
            ent = log.setdefault(b, [])
            if wr and not is_psum(b):
                ent[:] = [e for e in ent if not (lo <= e[0] and e[1] <= hi)]
            ent.append((lo, hi, wr, i))

    def run(q, fn, reads, writes, cost, sem=None, inc=1, lat=0.0):
        nodes.append([q, fn, sem if sem else qsem[q], inc, cost, lat, {}, sem is None, ahead[0]])
        i = len(nodes) - 1
        touch(i, reads, False)
        touch(i, writes, True)
        note(i, reads, False)
        note(i, writes, True)
        return i

    def landed(b, s, val, after, lat):
        nodes.append([None, None, s, val, 0.0, lat, {after: True}, False, 0.0])
        note(len(nodes) - 1, [(b, 0, 1 << 20)], True)

    def plan():
        n = len(nodes)
        succ = [[] for _ in range(n)]
        left = [len(nd[6]) for nd in nodes]
        for i, nd in enumerate(nodes):
            for j, w in nd[6].items():
                succ[j].append((i, w))
        way = [0.0] * n
        for i in range(n - 1, -1, -1):
            way[i] = nodes[i][4] + nodes[i][5] + max([way[k] + (WAKE if w else 0.0) for k, w in succ[i]] + [0.0])
        for i, nd in enumerate(nodes):
            way[i] += nd[8]
        ready = {q: [] for q in queue}
        free = {q: 0.0 for q in queue}
        at = [0.0] * n
        out = []

        def opened(i):
            if nodes[i][0] is None:
                done(i, at[i])
            else:
                ready[nodes[i][0]].append(i)

        def done(i, start):
            fin = start + nodes[i][4]
            for k, w in succ[i]:
                if w:
                    at[k] = max(at[k], fin + nodes[i][5] + (WAKE if nodes[k][0] is not None else 0.0))
                left[k] -= 1
                if left[k] == 0:
                    opened(k)
        for i in range(n):
            if not nodes[i][6]:
                opened(i)
        while True:
            best = None
            for q, lst in ready.items():
                if not lst:
                    continue
                first = min(max(at[i], free[q]) for i in lst)
                i = max([i for i in lst if max(at[i], free[q]) <= first + 0.02], key=lambda i: (way[i], -i))
                if best is None or first < best[0]:
                    best = (first, q, i)
            if best is None:
                return out
            q, i = best[1], best[2]
            start = max(at[i], free[q])
            free[q] = start + nodes[i][4]
            ready[q].remove(i)
            out.append(i)
            done(i, start)

    def issue():
        total, val, know, known = {}, {}, {}, {q: {} for q in queue}
        for i, nd in enumerate(nodes):
            if nd[0] is None:
                total[nd[2]] = total.get(nd[2], 0) + nd[3]
                val[i], know[i] = total[nd[2]], {}
        for i in plan():
            q, fn, s, inc = nodes[i][:4]
            deps = [j for j, w in nodes[i][6].items() if w]
            best = {}
            for j in deps:
                sj = nodes[j][2]
                if known[q].get(sj, 0) < val[j]:
                    best[sj] = max(best.get(sj, 0), val[j])
            for j in deps:
                for sk, vk in know[j].items():
                    if best.get(nodes[j][2]) == val[j] and sk in best and sk != nodes[j][2] and best[sk] <= vk:
                        del best[sk]
            for sk, vk in best.items():
                queue[q].wait_ge(T.sem[sk], vk)
                known[q][sk] = max(known[q].get(sk, 0), vk)
            for j in deps:
                for sk, vk in know[j].items():
                    known[q][sk] = max(known[q].get(sk, 0), vk)
            total[s] = total.get(s, 0) + inc
            val[i] = total[s]
            ins = fn(queue[q])
            if ins is not None:
                ins.then_inc(T.sem[s], inc)
            know[i] = dict(known[q])
        for s, x in total.items():
            if known["G"].get(s, 0) < x:
                g.wait_ge(T.sem[s], x)
    return run, landed, issue, ahead


def rank_program(g, core, T, topo):
    rank = T.rank_of(core)
    if rank is None:
        return
    run, landed, issue, ahead = make_tools(g, T)
    cores = list(T.cores)

    def size(b):
        n = 1
        for d in SCRATCH[b][1][1:]:
            n *= d
        return n

    def v(b, lo=0, hi=None, st=1):
        if b in PART:
            b, o, w = PART[b]
            lo, hi = o + lo, o + (w if hi is None else hi)
        elif len(SCRATCH[b][1]) == 3:
            return (T[b][:], [(b, 0, size(b))], size(b))
        hi = size(b) if hi is None else hi
        return (T[b][:, lo:hi] if st == 1 else T[b][:, lo:hi:st], [(b, lo, hi)], len(range(lo, hi, st)))

    def v3(b, i, lo, hi):
        m, w = SCRATCH[b][1][1:]
        if not isinstance(i, int):
            i0, i1 = (0, m) if i is None else i
            return (T[b][:, i0:i1, lo:hi], [(b, k * w + lo, k * w + hi) for k in range(i0, i1)], (i1 - i0) * (hi - lo))
        return (T[b][:, i, lo:hi], [(b, i * w + lo, i * w + hi)], hi - lo)

    def vp(lo, hi, st=1):
        return (T.ps_p[:, 0, lo:hi] if st == 1 else T.ps_p[:, 0, lo:hi:st], [("ps_p", lo, hi)], len(range(lo, hi, st)))

    def at(b, o):
        return (T[b][:].indirect(o[0]), [(b, 0, size(b))] + o[1], 16 * o[2], True)

    def isv(x):
        return isinstance(x, tuple)

    def regs(*xs):
        out = []
        for x in xs:
            if isv(x):
                out += x[1]
        return out

    def ap(x):
        return x[0] if isv(x) else x

    def wide(*xs):
        return any(SCRATCH[x[1][0][0]][2] in (F32, I32) for x in xs)

    def ts(o, a, s1, op0, s2=None, op1=None):
        if op1 is None:
            f = lambda e: e.tensor_scalar(out=o[0], in0=a[0], scalar1=ap(s1), scalar2=None, op0=op0)
        else:
            f = lambda e: e.tensor_scalar(out=o[0], in0=a[0], scalar1=ap(s1), scalar2=ap(s2), op0=op0, op1=op1)
        run("V", f, regs(a, s1, s2), regs(o), 0.05 + max(64, o[2] * (1.0 if wide(o, a) else 0.5)) * CY)

    def tt(o, a, b, op):
        k = 1.5 if len(a) > 3 else 1.0 if any(is_psum(x[1][0][0]) for x in (a, b)) else 2.0
        run("V", lambda e: e.tensor_tensor(out=o[0], in0=a[0], in1=b[0], op=op), regs(a, b), regs(o), 0.05 + max(64, o[2] * k) * CY)

    def tc(o, a):
        f = lambda e: e.tensor_copy(out=o[0], in_=a[0])
        if len(o) > 3:
            run("V", f, regs(a) + o[1][1:], o[1][:1], 0.05 + 3.8 * o[2] * CY)
        else:
            k = 1.5 if len(a) > 3 else 1.0 if wide(o, a) else 0.5
            run("V", f, regs(a), regs(o), 0.05 + max(64, o[2] * k) * CY)

    def fill(o, c):
        run("V", lambda e: e.memset(o[0], c), [], regs(o), 0.05 + o[2] * CY * (1.0 if wide(o) else 0.5))

    def vtr(o, a):
        run("V", lambda e: e.transpose(out=o[0], in_=a[0]), regs(a), regs(o), 0.05 + o[2] * CY)

    def scan(o, m, a):
        run("V", lambda e: e.tensor_tensor_scan(out=o[0], data0=m[0], data1=a[0], initial=0.0, op0=OP.mult, op1=OP.max), regs(m, a), regs(o), FX + o[2] * CY)

    def act(o, a, func, scale=1.0, bias=0.0, accum=None):
        b0, s0 = ap(bias), ap(scale)
        if accum is None:
            f = lambda e: e.activation(out=o[0], in_=a[0], func=func, bias=b0, scale=s0)
        else:
            f = lambda e: e.activation(out=o[0], in_=a[0], func=func, bias=b0, scale=s0, accum_out=accum[0])
        run("S", f, regs(a, bias, scale), regs(o, accum), 0.065 + max(64, o[2] * (1.5 if len(a) > 3 else 1.0)) * CY)

    def mm(o, lT, r, start, stop):
        k = 4.0 if SCRATCH[lT[1][0][0]][2] == F32 else 1.0
        run("T", lambda e: e.matmul(out=o[0], lhsT=lT[0], rhs=r[0], start=start, stop=stop), regs(lT, r), regs(o), 0.00071 * k * max(64, o[2]))

    def iota(o, pattern, base, cm):
        if SCRATCH[o[1][0][0]][2] != I32:
            f = lambda e: e.iota(o[0], pattern, base, cm, allow_small_or_imprecise_dtypes=True)
        else:
            f = lambda e: e.iota(o[0], pattern, base, cm)
        run("G", f, [], regs(o), 0.13 + 2 * o[2] * CY)

    def asel(o, a, pattern, cmp, base, cm):
        run("G", lambda e: e.affine_select(out=o[0], in_=a[0], pattern=pattern, compare_op=cmp, fill=0.0, base=base, channel_multiplier=cm), regs(a), regs(o), 0.17 + 2 * o[2] * CY)

    def send(src, dst, to, frm, kind):
        rid, pid = topo.addr(to)[:2]
        m = topo.mask(core, to)
        rs, ls = "r" + kind, "l" + kind

        def f(e):
            e.remote_dma(out_ap=T[dst][:], in_ap=T[src][:], remote_sem=T.sem[rs], local_sem=T.sem[ls], pid=pid, routing_id=rid, dma_engine_mask=m)
        i = run("G", f, [(src, 0, size(src))], [], 0.1, sem=ls, inc=len(topo.engines(core, to)))
        landed(dst, rs, len(topo.engines(frm, core)), i, HOP)

    run("Y", lambda e: e.dma_start(T.ENT[:], T.ent[:]), [], regs(v("ENT")), 0.1, "dEnt", 16, 5.0)
    run("S", lambda e: e.dma_start(T.wtS[:], T.wt[:]), [], regs(v("wtS")), 0.1, "dW", 16, 2.0)
    run("S", lambda e: e.dma_start(T.kapS[:], T.kap[:]), [], regs(v("kapS")), 0.1, "dK", 16, 2.0)

    def load(q, buf, par, sem):
        def f(e):
            for a in range(4):
                for h in range(2):
                    e.dma_start(T[buf][32 * a + 16 * h:32 * a + 16 * h + 16, 0:NM], T.feat[32 * a + 16 * par:32 * a + 16 * par + 16, :]).then_inc(T.sem[sem], 16)
        run(q, f, [], [(buf, 0, NM)], 0.8, sem, 128, 8.0)
    load("Y", "FA", 0, "dFA")
    load("S", "FB", 1, "dFB")

    fill(v("ones"), 1.0)
    fill(v("FA", NM, NM + 16), 0.0)
    fill(v("FB", NM, NM + 16), 0.0)
    fill(v("Np", S, SW_), 0.0)
    fill(v("Wp", S, SW_), 0.0)
    fill(v("Ip", S, SW_), 0.0)
    fill(v("ZE"), 0.0)
    fill(v("MK"), 1.0)
    fill(v("MK", 0, 128, 16), 0.0)
    fill(v("SC"), 0.0)
    fill(v("IX"), 0.0)
    for t in range(RO):
        fill(v("nab%d" % t, L, L + 8), 0.0)

    def slot(k, n=1):
        return v("CT", 128 * k, 128 * (k + n))
    iota(v("pidx"), [[0, 1]], 0, 1)
    iota(v("c64"), [[37, 64]], 0, 0)
    iota(v("io1"), [[1, 16]], 0, 0)
    iota(v("io16"), [[16, 16]], S, 0)
    asel(slot(10), v("ones"), [[-16, 8], [0, 16]], OP.is_ge, 0, 1)
    asel(slot(11), slot(10), [[16, 8], [0, 16]], OP.is_ge, 15, -1)
    asel(slot(12), v("ones"), [[-1, 128]], OP.is_equal, 0, 1)
    for p in range(2):
        asel(slot(p), v("ones"), [[-32, 4], [0, 2], [-1, 16]], OP.is_equal, -16 * p, 1)
    for p in range(2):
        for h in range(2):
            k = 2 + 2 * (2 * p + h)
            asel(slot(k), v("ones"), [[-32, 4], [-1000 if p == 0 else 1000, 2], [0, 16]], OP.is_ge, -16 * h - (1000 if p else 0), 1)
            asel(slot(k + 1), slot(k), [[32, 4], [0, 2], [0, 16]], OP.is_ge, 15 + 16 * h, -1)
    for h in range(2):
        for p in range(2):
            asel(slot(13 + 2 * h + p), v("ones"), [[-32, 4], [984, 2], [-1, 16]], OP.is_equal, 16 * (p - h) - 1000 * p, 1)
    iota(v("PI"), [[1, S]], 0, 0)
    tc(v("wtF"), v("wtS"))
    tc(v("kapF"), v("kapS"))
    for p in range(2):
        mm(vp(p, p + 1), slot(p), v("wtF"), True, True)
    tc(v("wcol"), vp(0, 2))
    for p in range(2):
        for h in range(2):
            k = 2 * p + h
            ts(v("WL", 128 * k, 128 * k + 128), slot(2 + 2 * k + 1), v("wcol", p, p + 1), OP.mult)
    ts(v("pm"), v("pidx"), 15, OP.bitwise_and)
    tc(v("pmF"), v("pm"))
    ts(v("p0"), v("pmF"), 0.0, OP.is_equal)
    ts(v("kcol"), v("pmF"), -2048.0, OP.mult, 15.0 * 2048, OP.add)
    ts(v("LL"), v("io16"), v("pmF"), OP.add)
    ts(v("ucol"), v("io1"), v("pmF"), OP.is_gt)
    for x in range(1, 16):
        act(v("UT", 128 * x, 128 * x + 128), slot(11), AF.Copy, scale=v("ucol", x, x + 1))
    ts(v("SEL0"), v("ones"), v("p0"), OP.mult)
    tc(v("BD"), slot(11))
    for q in range(8):
        act(v("SC", 16 * q, 16 * q + 129 * 15 + 1, 129), v("CT", 128 * 11 + 16 * q, 128 * 11 + 16 * q + 16), AF.Copy, scale=32768.0)
        tc(v("IX", 16 * q, 16 * q + 129 * 15 + 1, 129), v("CT", 128 * 12 + 16 * q, 128 * 12 + 16 * q + 16))
    tc(v("SWP"), slot(13, 4))
    tc(v("IDH"), slot(12))
    ts(v("c64b"), v("c64"), 63, OP.bitwise_and)
    ts(v("CC", 0, 64), v("c64b"), 4096.0, OP.mult, -262144.0 - 2033.0, OP.add)
    n = 64
    while n < S:
        act(v("CC", n, 2 * n), v("CC", 0, n), AF.Copy)
        n *= 2

    def entries(o, x, tmp):
        ts(tmp, x, 2047, OP.add)
        ts(tmp, tmp, -2048, OP.bitwise_and)
        tt(o, x, tmp, OP.add)
    entries(v("ab0"), v("ENT", 0, S, 8), v("o1"))
    for k in range(NV):
        entries(v("Np", 512 * k, 512 * k + 512), v("ENT", 512 * k, 512 * k + 512), v("ENT2", 512 * k, 512 * k + 512))

    BIG, MID = 12582912.0, 8387584.0

    for k in range(NV, 4):
        lo, hi = 512 * k, 512 * k + 512
        num, quo, bank = v("OR", S + lo, S + hi), v("OR", lo, hi), v("ps_u" if k == 2 else "ps_d")
        tc(num, v("ENT", lo, hi))
        act(quo, num, AF.Identity, scale=2.0 ** -11, bias=2047 / 4096)
        act(quo, quo, AF.Identity, bias=BIG)
        act(bank, quo, AF.Identity, scale=2048.0, bias=-2048.0 * BIG)
        tt(v("Np", lo, hi), num, bank, OP.add)

    def mid(o, x):
        act(o, x, AF.Identity, bias=-MID)

    def w_of(o, x, tmp):
        act(tmp, x, AF.Identity, scale=1 / 16, bias=-2056.5 / 16)
        act(tmp, tmp, AF.Identity, bias=BIG)
        act(o, tmp, AF.Identity, bias=MID / 16 - BIG)

    def n32_of(o, x, tmp):
        act(tmp, x, AF.Identity, scale=1 / 32, bias=-2048.5 / 32)
        act(tmp, tmp, AF.Identity, bias=BIG)
        act(tmp, tmp, AF.Identity, bias=-BIG)
        act(o, tmp, AF.Identity, scale=32.0, bias=MID + 2033)

    back = None
    for t in range(RO):
        clock = C0 + t
        thr = clock - 5
        d = 1 + t % 3
        to, frm = cores[(rank + d) % 4], cores[(rank - d) % 4]
        ab, aL, eb, eL, nab, naL = ["%s%d" % (x, t) for x in ("ab", "aL", "eb", "eL", "nab", "naL")]
        prev = "naL%d" % (t - 1)

        lanes = v("Np", t, S, 8) if t else v("ab0")
        ts(v("s1"), lanes, -2033, OP.add)
        act(v("nf"), lanes, AF.Identity, scale=2.0 ** -12, bias=BIG)
        act(v("nf"), v("nf"), AF.Identity, bias=-BIG - 1 - 2048)
        if t:
            act(v(ab), lanes, AF.Copy)
        send(ab, aL, to, frm, "a%d" % t)
        ts(v("lo1"), v("s1"), 31, OP.bitwise_and)
        dm = v3("pC", 0, 0, L)
        ts(dm, v("lo1"), 16, OP.is_lt, 8192.0, OP.mult)
        tt(v("idx"), v("nf"), dm, OP.add)
        vtr(v("TT"), v("idx"))
        for b in range(8):
            mm(v("ps_s%d" % (b // 4), b % 4, 128, 4), v("IDH"), v("TT", 32 * b, 32 * b + 32), True, True)
        for s in range(2):
            ts(v("LS", 128 * s, 128 * s + 128), v("ps_s%d" % s, 0, 128), 2048.0, OP.add, 4096.0, OP.min)
        if t:
            back(t - 1)
        for s in range(2):
            lo, hi = 128 * s, 128 * s + 128
            ahead[0] = AH1 if s == 0 else 0.0
            for k in range(8):
                for p in range(2):
                    o = 256 * s + 128 * p
                    acc = v("AC", o, o + 128)
                    win = at("FB" if p else "FA", v("LS", lo + 64 * p + 8 * k, lo + 64 * p + 8 * k + 8))
                    if k == 0:
                        act(acc, win, AF.Copy)
                    else:
                        tt(acc, win, acc, OP.max)
            for p in range(2):
                o = 256 * s + 128 * p
                tt(v("Y", lo + 64 * p, lo + 64 * p + 64), v("AC", o, o + 64), v("AC", o + 64, o + 128), OP.max)
            for h in range(2):
                for p in range(2):
                    k = 2 * p + h
                    mm(v("ps_u", lo + 64 * h, lo + 64 * h + 64), v("WL", 128 * k, 128 * k + 128), v("Y", lo + 64 * p, lo + 64 * p + 64), p == 0, p == 1)
            tc(v("ui", lo, hi), v("ps_u", lo, hi))
            ts(v("um", lo, hi), v("ui", lo, hi), 4095, OP.bitwise_and)
            tt(v("sq", lo, hi), v("um", lo, hi), v("um", lo, hi), OP.mult)
            ku = v3("pC", 0, lo, hi)
            if t:
                ts(ku, v("um", lo, hi), v("kapF", 0, 1), OP.mult, v(prev, L, L + 1), OP.add)
            else:
                ts(ku, v("um", lo, hi), v("kapF", 0, 1), OP.mult)
            ts(v("sq5", lo, hi), v("sq", lo, hi), 5, OP.arith_shift_right)
            tt(v("es", lo, hi), v("sq5", lo, hi), ku, OP.add)
            ts(v("e2", lo, hi), v("es", lo, hi), 2047, OP.bitwise_and)
            for h in range(2):
                tc(v3("%s%d" % (eb, s), None, 16 * h, 16 * h + 16), v("e2", lo + 64 * h, lo + 64 * h + 64))
            send("%s%d" % (eb, s), "%s%d" % (eL, s), to, frm, "e%d%d" % (t, s))
            ahead[0] = 0.0

        if t == 0:
            for k in range(WV):
                lo, hi = 512 * k, 512 * k + 512
                ts(v("ENT", lo, hi), v("Np", lo, hi), -2049, OP.add)
                ts(v("ENT2", lo, hi), v("ENT", lo, hi), 4, OP.arith_shift_right)
                ts(v("Wp", lo, hi), v("ENT2", lo, hi), -128.0, OP.max)
            for k in range(WV, 4):
                lo, hi = 512 * k, 512 * k + 512
                mid(v("OR", lo, hi), v("Np", lo, hi))
                w_of(v("Wp", lo, hi), v("OR", lo, hi), v("OR", lo, hi))
        else:
            act(v("Np", t - 1, S, 8), v(prev, 0, L), AF.Copy)
            mid(v("wn"), v(prev, 0, L))
            w_of(v("Wp", t - 1, S, 8), v("wn"), v("wn"))
            tc(at("Np", v("PL")), v("nb"))
            tc(at("Wp", v("PL")), v("wnb"))
        mid(v("fa"), v(aL))
        w_of(v("wf"), v("fa"), v("fw"))
        for m in range(16):
            act(v("OR", m, 4096, 16), v("wf"), AF.Copy)

        def side(x, k, s):
            lo, hi = 128 * s, 128 * s + 128
            far = v3("pB" if s else "pA", 1 - k, 0, 128)
            tt(v3("pC", k, lo, hi), v3("z", k, lo, hi), far, OP.is_le)
            tt(v3("X1", k, lo, hi), x, v3("pC", k, lo, hi), OP.mult)
            tt(far, x, far, OP.mult)
            act(v3("e0", k, lo, hi), v3("X1", k, lo, hi), AF.Relu, scale=-2.0 ** -18, bias=2.0 ** -18)

        act(v("ps_s0", L, 2 * L), v("CC", t, S, 8), AF.Copy)
        tt(v3("si", 0, 0, L), v(aL), v("ps_s0", L, 2 * L), OP.add)
        ts(v3("z", 0, 0, L), v3("si", 0, 0, L), 7 << 15, OP.bitwise_and)
        n32_of(v("ps_d", L, 2 * L), v("fa"), v("fl"))
        tt(v("lo"), v(aL), v("ps_d", L, 2 * L), OP.subtract)
        act(v("sg"), v("lo"), AF.Sign, bias=0.5 - thr)
        act(v("sh"), v("lo"), AF.Sign, bias=-15.5)
        act(v3("c", 0, 0, L), v("lo"), AF.Identity, scale=-1.0, bias=float(clock))
        for s in range(2):
            act(v3("pB" if s else "pA", 1, 0, 128), v("sg", 128 * s, 128 * s + 128), AF.Relu, scale=262144.0)
            act(v3("pB" if s else "pA", 3, 0, 128), v("sh", 128 * s, 128 * s + 128), AF.Relu, scale=float(thr))
            side(v(aL, 128 * s, 128 * s + 128), 0, s)
        for s in range(2):
            ts(v("kc", 128 * s, 128 * s + 128), v("%s%d" % (eL, s)), v("kcol", 0, 1), OP.add)
        for k in range(NCH):
            lo, hi, n = CW * k, CW * k + CW, CW // 16
            q = k * n
            ahead[0] = AH2 if k < NCH // 2 else 0.0
            tt(v("D", lo, hi), at("Wp", v("%s%d" % (eL, q // 128), q % 128, q % 128 + n)), v("OR", lo, hi), OP.subtract)
            act(v("A1", lo, hi), v("D", lo, hi), AF.Abs)
            act(v("B1", lo, hi), v("A1", lo, hi), AF.Abs, bias=-64.0)
            ts(v("IN", lo, hi), v("B1", lo, hi), 63.5, OP.is_lt)
            for m in range(16):
                mm(v("ps_s%d" % (q // 128), q % 128, q % 128 + n), v("SC", 128 * m, 128 * m + 128), v("IN", lo + m, hi, 16), m == 0, m == 15)
        for s in range(2):
            lo, hi = 128 * s, 128 * s + 128
            ahead[0] = AH3 if s == 0 else 0.0

            def f(b, n, o=0, st=1):
                return v(b, n * s + o, n * s + n, st)
            tt(f("key", 128), v("ps_s%d" % s, 0, 128), f("kc", 128), OP.add)
            vtr(f("TK", 128), f("key", 128))
            scan(f("k4", 128), v("MK"), f("TK", 128))
            ts(f("k5", 8), f("k4", 128, 15, 16), 2047, OP.bitwise_and)
            tc(f("pf", 8), f("k5", 8))
            for h in range(2):
                for p in range(2):
                    k = 2 * h + p
                    mm(vp(8 * s + h, 8 * s + 8, 2), v("SWP", 128 * k, 128 * k + 128), f("pf", 8, p, 2), p == 0, p == 1)
            tc(f("pl", 8), vp(8 * s, 8 * s + 8))
            act(f("P1", 8), vp(8 * s, 8 * s + 8), AF.Copy)
            act(f("P1n", 8), f("P1", 8), AF.Copy, scale=-1.0)
            act(f("CP", 128), at("CC", f("pl", 8)), AF.Copy)
            act(f("bx", 128), at("Np", f("pl", 8)), AF.Copy)
            tc(f("PB", 128), at("PI", f("pl", 8)))
            P, low = "pB" if s else "pA", f("lob", 128)
            tt(v3("si", 1, lo, hi), at("Np", f("pl", 8)), f("CP", 128), OP.add)
            ts(low, v3("si", 1, lo, hi), 31, OP.bitwise_and)
            ts(v3("z", 1, lo, hi), v3("si", 1, lo, hi), 7 << 15, OP.bitwise_and)
            ts(v3(P, 0, 0, 128), low, thr, OP.is_ge, 262144.0, OP.mult)
            ts(v3(P, 2, 0, 128), low, 16, OP.is_ge, float(thr), OP.mult)
            ts(v3("c", 1, lo, hi), low, -1.0, OP.mult, float(clock), OP.add)
            side(f("bx", 128), 1, s)
            a = v3("X1", 0, lo, hi)
            tt(f("dd", 128), a, f("bx", 128), OP.subtract)
            act(f("dq", 128), f("dd", 128), AF.Square, scale=2.0 ** -11)
            ts(f("sm", 128), f("dq", 128), 1.0, OP.is_lt)
            tt(f("sm", 128), f("sm", 128), v3("pC", 1, lo, hi), OP.mult)
            both, big = v3(P, (2, 4), 0, 128), v3(P, 3, 0, 128)
            tt(v3(P, 2, 0, 128), f("lo", 128), v3(P, 2, 0, 128), OP.is_lt)
            tt(big, low, big, OP.is_lt)
            tt(both, v3("c", None, lo, hi), both, OP.mult)
            tt(f("XH", 128), a, v3(P, 2, 0, 128), OP.add)
            tt(big, f("bx", 128), big, OP.add)
            tt(big, f("XH", 128), big, OP.max)
            tt(big, f("sm", 128), big, OP.mult)
            fil = v3(P, (0, 2), 0, 128)
            tt(fil, v3("e0", None, lo, hi), fil, OP.mult)
            tt(v3("M", None, lo, hi), v3("X1", None, lo, hi), fil, OP.max)
            tt(f("nb", 128), v3("M", 1, lo, hi), big, OP.max)
        ahead[0] = 0.0
        act(v("PBf", 128, L), at("PI", v("pl", 8, 16)), AF.Copy)
        for c in range(16):
            n = 256 - 16 * c
            if c < EQV:
                ts(v3("EQ", c, 0, n), v("PB", 16 * c, 256), v("P1", c, c + 1), OP.is_equal)
            else:
                act(v3("EA", c - EQV, 0, n), v("PBf", 16 * c, 256), AF.Abs, bias=v("P1n", c, c + 1))
                act(v3("EQ", c, 0, n), v3("EA", c - EQV, 0, n), AF.Relu, scale=-1.0, bias=1.0)
        mm(v("ps_d", 0, 256), v("BD"), v("ZE"), True, False)
        for c in range(15):
            mm(v("ps_d", 16 * c + 16, 256), v("BD"), v3("EQ", c, 16, 256 - 16 * c), False, False)
        for x in range(1, 16):
            col = (T.EQ[:, 0:16, x], [("EQ", 256 * c + x, 256 * c + x + 1) for c in range(16)], 16)
            mm(v("ps_d", x, 256, 16), v("UT", 128 * x, 128 * x + 128), col, False, x == 15)
        act(v("lose"), v("ps_d", 0, 256), AF.Sign, accum=v("lc"))
        for x in range(16):
            mm(v("ps_d", 256, 272), v("IX", 128 * x, 128 * x + 128), v("lose", x, 256, 16), x == 0, x == 15)
        tt(v("t16"), v("LL"), v("ps_d", 256, 272), OP.mult)
        tt(v("u16"), v("t16"), v("P1"), OP.max)
        tc(v("PL"), v("u16"))
        if t < RO - 1:
            mm(v3("ps_p", 2, 0, 1), v("SEL0"), v("lc"), True, True)

        def back(t, aL=aL, nab=nab, to=to, frm=frm, naL=naL):
            na, df = v3("pC", 0, 0, L), v3("pC", 1, 0, L)
            for s in range(2):
                tt(v3("pC", 0, 128 * s, 128 * s + 128), v3("M", 0, 128 * s, 128 * s + 128), v3("pB" if s else "pA", 3, 0, 128), OP.max)
            tt(df, v(aL), na, OP.subtract)
            tt(v("na"), v("lose"), df, OP.mult)
            tt(v(nab, 0, L), v("na"), na, OP.add)
            if t < RO - 1:
                act(v("an"), v3("ps_p", 2, 0, 1), AF.Copy, scale=-1.0)
                act(v("aq"), v("an"), AF.Identity, scale=1 / 32, bias=-15.5 / 32)
                act(v("aq"), v("aq"), AF.Identity, bias=BIG)
                act(v("aq"), v("aq"), AF.Identity, bias=-BIG)
                act(v(nab, L, L + 1), v("aq"), AF.Identity, scale=-32.0, bias=v("an"))
            send(nab, naL, frm, to, "n%d" % t)
            if t < RO - 1:
                mid(v("wn"), v("nb"))
                w_of(v("wnb"), v("wn"), v("wn"))

        if t == RO - 1:
            back(t)
        else:
            tc(at("Np", v("PL")), v("nb"))

    for k in range(4):
        lo, hi = 512 * k, 512 * k + 512
        bank = v(("ps_u", "ps_s0", "ps_s1", "ps_u")[k])
        act(v("OR", lo, hi), v("Np", lo, hi), AF.Identity, scale=2.0 ** -12, bias=BIG)
        act(bank, v("OR", lo, hi), AF.Identity, scale=2048.0, bias=-2048.0 * BIG)
        tt(v("Ip", lo, hi), v("Np", lo, hi), bank, OP.subtract)

    def number(o, x):
        ts(v("o1"), x, 2047, OP.add)
        ts(v("o2"), v("o1"), 1, OP.arith_shift_right, -2048, OP.bitwise_and)
        tt(o, x, v("o2"), OP.subtract)
    number(v("nbc"), v("nb"))
    number(v("Ip", RO - 1, S, 8), v("naL%d" % (RO - 1), 0, L))
    tc(at("Ip", v("PL")), v("nbc"))
    run("Y", lambda e: e.dma_start(T.yent[:], T.Ip[:, 0:S]), regs(v("Ip", 0, S)), [("yent", 0, S)], 0.1, "dY", 16, 6.0)
    issue()
